import numpy as np
import ml_dtypes


def mxq(x, axis, fmt="e4m3"):
    dtype, down = {"e4m3": (ml_dtypes.float8_e4m3fn, 7), "e5m2": (ml_dtypes.float8_e5m2, 14)}[fmt]
    v = np.moveaxis(np.asarray(x, np.float32).astype(ml_dtypes.bfloat16).astype(np.float64), axis, -1)
    blocks = v.reshape(v.shape[:-1] + (-1, 32))
    amax = np.abs(blocks).max(-1, keepdims=True)
    byte = np.maximum(np.where(amax > 0, np.frexp(amax)[1] - 1 + 127, 0) - down, 1)
    scale = np.exp2(byte - 127.0)
    codes = (blocks / scale).astype(np.float32).astype(dtype).astype(np.float64)
    return np.moveaxis((codes * scale).reshape(v.shape), -1, axis)


WIDE = False


def mx_kscale(k):
    if not WIDE:
        return np.ones(k)
    levels = np.array([10, -10, 5, -5, 0])
    if k % 512:
        return np.exp2(np.random.permutation(np.resize(levels, k // 32))).repeat(32)
    a = np.empty((k // 512, 16))
    for p in range(k // 512):
        a[p, :8] = np.random.permutation(np.resize(levels, 8))
        for g in range(8):
            far = levels[np.abs(levels - a[p, g]) >= 10]
            a[p, g + 8] = far[np.random.randint(len(far))]
    return np.exp2(a.ravel()).repeat(32)


BF16 = ml_dtypes.bfloat16


def bf(x):
    return np.asarray(x, np.float32).astype(BF16)


def f64(x):
    return np.asarray(x).astype(np.float64)

def planes(Y):
    n, m = Y.shape
    b = f64(bf(Y)).reshape(n // 32, 32, m)
    amax = np.abs(b).max(1)
    byte = np.clip(np.where(amax > 0, np.frexp(amax)[1] - 1 + 127 - 7, 1), 1, 254)
    codes = (b * np.exp2(127.0 - byte)[:, None, :]).reshape(n, m).astype(np.float32).astype(ml_dtypes.float8_e4m3fn).view(np.uint8)
    words = codes.reshape(n // 512, 128, 4, m).transpose(0, 1, 3, 2)
    return np.ascontiguousarray(words), np.ascontiguousarray(byte.astype(np.uint8).reshape(n // 512, 16, m))


T, D, E = 1536, 1024, 2048


def setup_inputs():
    s = mx_kscale(D)
    h = np.random.randn(T, D)
    spread = np.exp(0.6 * np.random.randn(E, 1))
    w_in = 0.8 * np.random.randn(E, D) * spread / np.sqrt(D)
    b_in = 0.5 * np.random.randn(E)
    return {
        "h": bf(h * s[None, :]),
        "w_in": bf(w_in / s[None, :]),
        "b_in": bf(b_in),
    }


def reference(h, w_in, b_in):
    hq = mxq(f64(h), 1, "e4m3")
    wq = mxq(f64(w_in), 1, "e4m3")
    a = (wq @ hq.T) + f64(b_in)[:, None]
    y = np.log(1.0 + np.exp(a))
    Y = y.reshape(E, T)
    words, scales = planes(Y)
    return y, words, scales

@@ -1,0 +1,313 @@
+from contextlib import ExitStack
+
+import concourse.mybir as mybir
+from concourse.masks import make_identity
+
+T, D, E = 1536, 1024, 2048
+FLOPS = 2 * T * D * E
+
+F32 = mybir.dt.float32
+BF16 = mybir.dt.bfloat16
+I32 = mybir.dt.int32
+U32 = mybir.dt.uint32
+U8 = mybir.dt.uint8
+FP8X4 = mybir.dt.float8_e4m3fn_x4
+ACT = mybir.ActivationFunctionType
+
+P = 128
+PACK = 4
+PASSES = 2
+CHUNK = 512
+CHUNKS = T // CHUNK
+GROUP = P * PACK
+GROUPS = E // GROUP
+BANKS = 8
+
+RAW_BUFS = 10
+SHUF_BUFS = 3
+GROUPED_BUFS = 4
+Y_BUFS = 3
+YBF_BUFS = 3
+
+HALF = 2 * P
+PAIRS = [(kind, i) for i in range(6) for kind in ("h", "w")] + [("w", 6), ("w", 7)]
+FIRST_PAIRS = 12
+WARM_UP = 5
+WARM_AFTER = [1, 1, 0, 0, 0, 0, 0, 0, 0, 0, 0, 0]
+HALVES_AFTER = [0, 0, 0, 2, 2, 4, 2, 6, 6, 4, 8, 0]
+LAG = 2
+EVAC = ["AA", "AA", "AA", "AA", "AV", "AV", "AV", "AV", "VV", "VV", "AV", "VV", "VV", "VV"]
+
+
+def w_pair(g, t):
+    return PAIRS.index(("w", 2 * g + t // 2))
+
+
+def h_pair(i):
+    return PAIRS.index(("h", i))
+
+
+def schedule():
+    steps = []
+    todo = [(g, t, i) for g in range(GROUPS) for t in range(PACK) for i in range(T // HALF)]
+    todo.sort(key=lambda x: (max(w_pair(x[0], x[1]), h_pair(x[2])), x))
+
+    def prepare(p):
+        steps.append(("turn", p, 0))
+        steps.append(("turn", p, 1))
+        if p + 1 < len(PAIRS):
+            steps.append(("shuffle", p + 1))
+        if p + RAW_BUFS < len(PAIRS):
+            steps.append(("load", p + RAW_BUFS))
+        if p > 0 and ("quant", p - 1, 1) not in steps:
+            steps.append(("quant", p - 1, 1))
+        steps.append(("evac", p, 0, EVAC[p][0]))
+        steps.append(("evac", p, 1, EVAC[p][1]))
+        steps.append(("quant", p, 0))
+
+    def multiply(halves, newest):
+        while halves > 0:
+            ready = [x for x in todo if max(w_pair(x[0], x[1]), h_pair(x[2])) <= newest]
+            whole = [x for x in ready if x[2] % 2 == 0 and (x[0], x[1], x[2] + 1) in ready]
+            g, t, i = (whole + ready)[0]
+            n = 2 if whole else 1
+            for j in range(n):
+                todo.remove((g, t, i + j))
+            steps.append(("mm", g, t, HALF * i, HALF * (i + n)))
+            steps.append(("exp", g, t, HALF * i, HALF * (i + n)))
+            halves -= n
+
+    def planes(g, cuts):
+        for i in range(len(cuts) - 1):
+            steps.append(("cast", g, cuts[i], cuts[i + 1]))
+            if i > 0:
+                steps.append(("quant_y", g, cuts[i - 1], cuts[i]))
+        steps.append(("quant_y", g, cuts[-2], cuts[-1]))
+
+    for p in range(RAW_BUFS):
+        steps.append(("load", p))
+    steps.append(("warm_prep",))
+    steps.append(("warm", -1, WARM_UP))
+    steps.append(("shuffle", 0))
+    for p in range(FIRST_PAIRS):
+        prepare(p)
+        if WARM_AFTER[p]:
+            steps.append(("warm", p, WARM_AFTER[p]))
+        if p < FIRST_PAIRS - 1:
+            multiply(HALVES_AFTER[p], p - LAG)
+    steps.append(("quant", FIRST_PAIRS - 1, 1))
+    multiply(len([x for x in todo if x[0] < GROUPS - 1]), FIRST_PAIRS - 1)
+    for p in range(FIRST_PAIRS, len(PAIRS)):
+        prepare(p)
+    steps.append(("quant", len(PAIRS) - 1, 1))
+
+    last = GROUPS - 1
+    for g in range(last):
+        for t in range(PACK):
+            for a, b in ([(0, CHUNK), (CHUNK, T)] if g == 0 and t == 0 else [(0, T)]):
+                steps.append(("ln", g, t, t + 1, a, b))
+                steps.append(("store_y", g, t, t + 1, a, b))
+        if g > 0:
+            steps.append(("store_words", g - 1, 0, T))
+            steps.append(("store_scales", g - 1, 0, T))
+        planes(g, [0, 512, 1024, 1536])
+    steps.append(("store_words", last - 1, 0, T))
+    steps.append(("store_scales", last - 1, 0, T))
+    multiply(len(todo), len(PAIRS))
+
+    for c in range(CHUNKS):
+        a, b = CHUNK * c, CHUNK * (c + 1)
+        for t0, t1 in ([(0, 1), (1, 2), (2, 4)] if c == 0 else [(0, 2), (2, 4)]):
+            steps.append(("ln", last, t0, t1, a, b))
+            steps.append(("store_y", last, t0, t1, a, b))
+        steps.append(("cast", last, a, b))
+        steps.append(("quant_y", last, a, b))
+        if c > 0:
+            steps.append(("store_words", last, a - CHUNK, a))
+    steps.append(("store_words", last, T - CHUNK, T))
+    steps.append(("store_scales", last, 0, T, "A"))
+    return steps
+
+
+def tile_ssm_channel_softplus_g2_kernel(tc, h, w_in, b_in, out_0, out_1, out_2):
+    nc = tc.nc
+    with ExitStack() as ctx:
+        sb = ctx.enter_context(tc.tile_pool(name="sb", bufs=1))
+        ps = ctx.enter_context(tc.psum_pool(name="ps", bufs=1))
+        ctx.enter_context(tc.manual_schedule())
+
+        bias_bf = sb.tile([P, GROUPS, PACK], BF16, name="bias_bf")
+        bias = sb.tile([P, GROUPS, PACK], F32, name="bias")
+        nc.scalar.dma_start(out=bias_bf[:], in_=b_in.rearrange("(g p t) -> p g t", p=P, t=PACK))
+
+        zero = sb.tile([P, 1], F32, name="zero")
+        exp_zero = sb.tile([P, 1], F32, name="exp_zero")
+        nc.vector.memset(zero[:], 0.0)
+        nc.scalar.activation(out=exp_zero[:], in_=zero[:], func=ACT.Exp)
+
+        ones = sb.tile([P, HALF * PACK], BF16, name="ones", align_bytes=64)
+        ones_codes = sb.tile([P, HALF], U32, name="ones_codes", align_bytes=64)
+        ones_scales = sb.tile([P, HALF], U8, name="ones_scales", align_bytes=64)
+
+        ident = sb.tile([P, P], F32, name="ident")
+        make_identity(nc, ident[:])
+        nc.gpsimd.tensor_copy(out=bias[:], in_=bias_bf[:])
+
+        h_codes = sb.tile([P, PASSES, T], U32, name="h_codes", align_bytes=64)
+        h_scales = sb.tile([P, PASSES, T], U8, name="h_scales", align_bytes=64)
+        w_codes = sb.tile([P, GROUPS * PACK, PASSES, P], U32, name="w_codes", align_bytes=64)
+        w_scales = sb.tile([P, GROUPS * PACK, PASSES, P], U8, name="w_scales", align_bytes=64)
+
+        words_hbm = out_1.rearrange("g p m t -> g p (m t)").bitcast(I32)
+        scales_hbm = out_2.bitcast(I32)
+
+        raw, shuf, turned, grouped, acc, y, y_bf, y_words, y_scales = {}, {}, {}, {}, {}, {}, {}, {}, {}
+        fills = []
+        casts = []
+
+        def next_bank():
+            tag = "bank%d" % (len(fills) % BANKS)
+            fills.append(tag)
+            return ps.tile([P, CHUNK], F32, name=tag, tag=tag)
+
+        def load(p):
+            kind, i = PAIRS[p]
+            tag = "raw%d" % (p % RAW_BUFS)
+            raw[p] = sb.tile([P, 2, D], BF16, name=tag, tag=tag)
+            if kind == "h":
+                src = h[2 * P * i : 2 * P * (i + 1), :].rearrange("(m s) k -> m s k", s=2)
+            else:
+                rows = w_in[GROUP * (i // 2) : GROUP * (i // 2 + 1), :].rearrange("(m t) k -> m t k", t=PACK)
+                src = rows[:, 2 * (i % 2) : 2 * (i % 2) + 2, :]
+            nc.sync.dma_start(out=raw[p][:], in_=src)
+
+        def shuffle(p):
+            tag = "shuf%d" % (p % SHUF_BUFS)
+            shuf[p] = sb.tile([P, 2, 2 * D // 32, 16], BF16, name=tag, tag=tag)
+            nc.vector.tensor_copy(out=shuf[p][:], in_=raw[p][:].rearrange("p s (j u i) -> p u (s j) i", u=2, i=16))
+
+        def turn(p, b):
+            kind, i = PAIRS[p]
+            words = shuf[p][:].rearrange("p u j i -> p (u j i)").bitcast(F32)
+            bank = next_bank()
+            turned[(p, b)] = bank
+            for o in range(2):
+                s, g = (o, b) if kind == "h" else (b, o)
+                for u in range(2):
+                    first = (u * 4 + s * 2 + g) * P
+                    col = (o * 2 + u) * P
+                    nc.tensor.transpose(bank[:, col : col + P], words[:, first : first + P], ident[:])
+
+        def evac(p, b, engine):
+            kind, i = PAIRS[p]
+            tag = "grouped%d" % ((2 * p + b) % GROUPED_BUFS)
+            tile = sb.tile([P, 2 * P * PACK], BF16, name=tag, tag=tag, align_bytes=64)
+            grouped[(p, b)] = tile
+            if kind == "h":
+                src = turned[(p, b)][:].rearrange("p (q m) -> p m q", m=P)
+                dst = tile[:].bitcast(F32).rearrange("p (m q) -> p m q", m=P)
+            else:
+                src = turned[(p, b)][:].rearrange("p (g u m) -> p g m u", u=2, m=P)
+                dst = tile[:].bitcast(F32).rearrange("p (g m u) -> p g m u", u=2, m=P)
+            if engine == "A":
+                nc.scalar.copy(out=dst, in_=src)
+            else:
+                nc.vector.tensor_copy(out=dst, in_=src)
+
+        def quant(p, b):
+            kind, i = PAIRS[p]
+            if kind == "h":
+                cols = slice(2 * P * i, 2 * P * (i + 1))
+                codes, scales = h_codes[:, b, cols], h_scales[:, b, cols]
+            else:
+                codes = w_codes[:, 2 * i + b, :, :].rearrange("p g m -> p (g m)")
+                scales = w_scales[:, 2 * i + b, :, :].rearrange("p g m -> p (g m)")
+            nc.vector.quantize_mx(out=codes.bitcast(FP8X4), scales=scales, in_=grouped[(p, b)][:])
+
+        def warm_prep():
+            nc.vector.memset(ones[:], 1.0)
+            nc.vector.quantize_mx(out=ones_codes[:].bitcast(FP8X4), scales=ones_scales[:], in_=ones[:])
+
+        def warm(p, n):
+            bank = next_bank()
+            for i in range(2 * n):
+                nc.tensor.matmul_mx(
+                    out=bank[:, 0:HALF],
+                    lhsT=ones_codes[:, 0:P].bitcast(FP8X4),
+                    lhsT_scale=ones_scales[:, 0:P],
+                    rhs=ones_codes[:].bitcast(FP8X4),
+                    rhs_scale=ones_scales[:],
+                    start=True,
+                    stop=True,
+                )
+
+        def mm(g, t, a, b):
+            bank = next_bank()
+            acc[(g, t, a)] = bank
+            cols = slice(a, b)
+            for k in range(PASSES):
+                nc.tensor.matmul_mx(
+                    out=bank[:, 0 : b - a],
+                    lhsT=w_codes[:, PACK * g + t, k, :].bitcast(FP8X4),
+                    lhsT_scale=w_scales[:, PACK * g + t, k, :],
+                    rhs=h_codes[:, k, cols].bitcast(FP8X4),
+                    rhs_scale=h_scales[:, k, cols],
+                    start=(k == 0),
+                    stop=(k == PASSES - 1),
+                )
+
+        def exp(g, t, a, b):
+            if g not in y:
+                tag = "y%d" % (g % Y_BUFS)
+                y[g] = sb.tile([P, PACK, T], F32, name=tag, tag=tag)
+            nc.scalar.activation(
+                out=y[g][:, t, a:b],
+                in_=acc[(g, t, a)][:, 0 : b - a],
+                func=ACT.Exp,
+                bias=bias[:, g, t : t + 1],
+            )
+
+        def ln(g, t0, t1, a, b):
+            part = y[g][:, t0:t1, a:b]
+            nc.scalar.activation(out=part, in_=part, func=ACT.Ln, bias=1.0)
+
+        def store_y(g, t0, t1, a, b):
+            rows = out_0[GROUP * g : GROUP * (g + 1), :].rearrange("(p t) m -> p t m", t=PACK)
+            nc.sync.dma_start(out=rows[:, t0:t1, a:b], in_=y[g][:, t0:t1, a:b])
+
+        def cast(g, a, b):
+            tag = "y_bf%d" % (len(casts) % YBF_BUFS)
+            casts.append(tag)
+            tile = sb.tile([P, CHUNK * PACK], BF16, name=tag, tag=tag, align_bytes=64)
+            y_bf[(g, a)] = tile
+            nc.vector.tensor_copy(
+                out=tile[:, 0 : (b - a) * PACK].rearrange("p (c i t) -> p c t i", i=4, t=PACK),
+                in_=y[g][:, :, a:b].rearrange("p t (c i) -> p c t i", i=4),
+            )
+
+        def quant_y(g, a, b):
+            if g not in y_words:
+                y_words[g] = sb.tile([P, T], U32, name="y_words%d" % g, align_bytes=64)
+                y_scales[g] = sb.tile([P, T], U8, name="y_scales%d" % g, align_bytes=64)
+            nc.vector.quantize_mx(
+                out=y_words[g][:, a:b].bitcast(FP8X4),
+                scales=y_scales[g][:, a:b],
+                in_=y_bf[(g, a)][:, 0 : (b - a) * PACK],
+            )
+
+        def store_words(g, a, b):
+            nc.sync.dma_start(out=words_hbm[g, :, a:b], in_=y_words[g][:, a:b].bitcast(I32))
+
+        def store_scales(g, a, b, engine="Q"):
+            queue = nc.scalar if engine == "A" else nc.sync
+            for q in range(4):
+                queue.dma_start(
+                    out=scales_hbm[g, 4 * q : 4 * q + 4, a // 4 : b // 4],
+                    in_=y_scales[g][32 * q : 32 * q + 4, a:b].bitcast(I32),
+                )
+
+        emit = {"load": load, "shuffle": shuffle, "turn": turn, "evac": evac, "quant": quant, "mm": mm, "warm": warm, "warm_prep": warm_prep, "exp": exp,
+                "ln": ln, "store_y": store_y, "cast": cast, "quant_y": quant_y, "store_words": store_words,
+                "store_scales": store_scales}
+        for step in schedule():
+            emit[step[0]](*step[1:])

@@ -23,59 +23,69 @@ GROUP = P * PACK
 GROUPS = E // GROUP
 BANKS = 8
 
-RAW_BUFS = 10
-SHUF_BUFS = 3
+RAW_BUFS = 20
+SHUF_BUFS = 6
 GROUPED_BUFS = 4
 Y_BUFS = 3
 YBF_BUFS = 3
 
-HALF = 2 * P
-PAIRS = [(kind, i) for i in range(6) for kind in ("h", "w")] + [("w", 6), ("w", 7)]
-FIRST_PAIRS = 12
-WARM_UP = 5
-WARM_AFTER = [1, 1, 0, 0, 0, 0, 0, 0, 0, 0, 0, 0]
-HALVES_AFTER = [0, 0, 0, 2, 2, 4, 2, 6, 6, 4, 8, 0]
-LAG = 2
-EVAC = ["AA", "AA", "AA", "AA", "AV", "AV", "AV", "AV", "VV", "VV", "AV", "VV", "VV", "VV"]
-
-
-def w_pair(g, t):
-    return PAIRS.index(("w", 2 * g + t // 2))
-
-
-def h_pair(i):
-    return PAIRS.index(("h", i))
+SHUFFLE = True
+PHASES = [("hhww" * 6, "wwww"), ("", "")]
+ORDER = "".join(x + y for x, y in PHASES)
+BLOCKS = [(c, ORDER[:i].count(c)) for i, c in enumerate(ORDER)]
+FIRST_BLOCKS = 24
+PLANES_AT = -1
+SINGLE_LOADS = 4
+WARM_UP = 16
+WARM_AFTER = [0, 0, 4, 4] + [0] * 20
+TILES_AFTER = [0, 0, 0, 0, 0, 0, 4, 0, 0, 8, 0, 0, 12, 0, 0, 12, 0, 0, 16, 0, 0, 16, 0, 0]
+LAG = 3
+AHEAD = 2
+QUANT_LAG = 1
+EVAC = list("AVAAAAAAAAAVAVAAVAVAVVAVVVVV")
 
 
 def schedule():
     steps = []
-    todo = [(g, t, i) for g in range(GROUPS) for t in range(PACK) for i in range(T // HALF)]
-    todo.sort(key=lambda x: (max(w_pair(x[0], x[1]), h_pair(x[2])), x))
+    h_at = [BLOCKS.index(("h", i)) for i in range(T // P)]
+    w_at = [BLOCKS.index(("w", i)) for i in range(E // P)]
+    todo = [(w, i) for w in range(E // P) for i in range(T // P)]
+    todo.sort(key=lambda x: (max(w_at[x[0]], h_at[x[1]]), x))
+
+    def load(p):
+        if p < SINGLE_LOADS:
+            steps.append(("load", p, 1))
+        elif p % 2 == 0 and p < len(BLOCKS):
+            steps.append(("load", p, 2))
+
+    def shuffle(p):
+        if SHUFFLE and p < len(BLOCKS):
+            steps.append(("shuffle", p, "V"))
 
     def prepare(p):
-        steps.append(("turn", p, 0))
-        steps.append(("turn", p, 1))
-        if p + 1 < len(PAIRS):
-            steps.append(("shuffle", p + 1))
-        if p + RAW_BUFS < len(PAIRS):
-            steps.append(("load", p + RAW_BUFS))
-        if p > 0 and ("quant", p - 1, 1) not in steps:
-            steps.append(("quant", p - 1, 1))
-        steps.append(("evac", p, 0, EVAC[p][0]))
-        steps.append(("evac", p, 1, EVAC[p][1]))
-        steps.append(("quant", p, 0))
+        steps.append(("turn", p))
+        shuffle(p + AHEAD)
+        load(p + RAW_BUFS - 1)
+        steps.append(("evac", p, EVAC[p]))
+        quant(p - QUANT_LAG)
 
-    def multiply(halves, newest):
-        while halves > 0:
-            ready = [x for x in todo if max(w_pair(x[0], x[1]), h_pair(x[2])) <= newest]
-            whole = [x for x in ready if x[2] % 2 == 0 and (x[0], x[1], x[2] + 1) in ready]
-            g, t, i = (whole + ready)[0]
-            n = 2 if whole else 1
+    def quant(p):
+        if p >= 0 and ("quant", p) not in steps:
+            steps.append(("quant", p))
+
+    def multiply(tiles, newest):
+        while tiles > 0:
+            ready = [x for x in todo if max(w_at[x[0]], h_at[x[1]]) <= newest]
+            for n in (4, 2, 1):
+                runs = [x for x in ready if x[1] % n == 0 and all((x[0], x[1] + j) in ready for j in range(n))]
+                if runs:
+                    break
+            w, i = runs[0]
             for j in range(n):
-                todo.remove((g, t, i + j))
-            steps.append(("mm", g, t, HALF * i, HALF * (i + n)))
-            steps.append(("exp", g, t, HALF * i, HALF * (i + n)))
-            halves -= n
+                todo.remove((w, i + j))
+            steps.append(("mm", w // PACK, w % PACK, P * i, P * (i + n)))
+            steps.append(("exp", w // PACK, w % PACK, P * i, P * (i + n)))
+            tiles -= n
 
     def planes(g, cuts):
         for i in range(len(cuts) - 1):
@@ -84,36 +94,69 @@ def schedule():
                 steps.append(("quant_y", g, cuts[i - 1], cuts[i]))
         steps.append(("quant_y", g, cuts[-2], cuts[-1]))
 
-    for p in range(RAW_BUFS):
-        steps.append(("load", p))
+    for p in range(RAW_BUFS - 1):
+        load(p)
     steps.append(("warm_prep",))
     steps.append(("warm", -1, WARM_UP))
-    steps.append(("shuffle", 0))
-    for p in range(FIRST_PAIRS):
-        prepare(p)
-        if WARM_AFTER[p]:
-            steps.append(("warm", p, WARM_AFTER[p]))
-        if p < FIRST_PAIRS - 1:
-            multiply(HALVES_AFTER[p], p - LAG)
-    steps.append(("quant", FIRST_PAIRS - 1, 1))
-    multiply(len([x for x in todo if x[0] < GROUPS - 1]), FIRST_PAIRS - 1)
-    for p in range(FIRST_PAIRS, len(PAIRS)):
-        prepare(p)
-    steps.append(("quant", len(PAIRS) - 1, 1))
-
+    for p in range(AHEAD):
+        shuffle(p)
     last = GROUPS - 1
-    for g in range(last):
-        for t in range(PACK):
-            for a, b in ([(0, CHUNK), (CHUNK, T)] if g == 0 and t == 0 else [(0, T)]):
+    logged = [0] * (E // P)
+    planed = [0] * GROUPS
+    stored = [0] * GROUPS
+
+    def make_planes():
+        for g in range(GROUPS):
+            upto = min(logged[PACK * g : PACK * (g + 1)])
+            if upto > planed[g]:
+                planes(g, list(range(planed[g], upto + 1, CHUNK)))
+                planed[g] = upto
+
+    def store_planes():
+        for g in range(GROUPS):
+            if planed[g] > stored[g]:
+                steps.append(("store_words", g, stored[g], planed[g]))
+                stored[g] = planed[g]
+                if planed[g] == T:
+                    steps.append(("store_scales", g, 0, T))
+
+    p = 0
+    for phase, (with_exp, with_ln) in enumerate(PHASES):
+        for kind in with_exp:
+            prepare(p)
+            if WARM_AFTER[p]:
+                steps.append(("warm", p, WARM_AFTER[p]))
+            multiply(TILES_AFTER[p], p - LAG)
+            if p == PLANES_AT:
+                quant(p)
+                make_planes()
+                store_planes()
+            p += 1
+        for q in range(p):
+            quant(q)
+        seen = ORDER[:p]
+        multiply(len([x for x in todo if x[0] < seen.count("w") and x[1] < seen.count("h")]), p - 1)
+        if phase == len(PHASES) - 1:
+            break
+        for kind in with_ln:
+            prepare(p)
+            p += 1
+        for q in range(p):
+            quant(q)
+        upto = P * seen.count("h")
+        first = True
+        for w in range(seen.count("w")):
+            g, t, a = w // PACK, w % PACK, logged[w]
+            for a, b in ([(a, a + CHUNK), (a + CHUNK, upto)] if first and upto > a + CHUNK else [(a, upto)]):
                 steps.append(("ln", g, t, t + 1, a, b))
                 steps.append(("store_y", g, t, t + 1, a, b))
-        if g > 0:
-            steps.append(("store_words", g - 1, 0, T))
-            steps.append(("store_scales", g - 1, 0, T))
-        planes(g, [0, 512, 1024, 1536])
-    steps.append(("store_words", last - 1, 0, T))
-    steps.append(("store_scales", last - 1, 0, T))
-    multiply(len(todo), len(PAIRS))
+            first = False
+            logged[w] = upto
+            if t == PACK - 1 and phase == len(PHASES) - 2:
+                store_planes()
+                make_planes()
+        if phase == len(PHASES) - 2:
+            store_planes()
 
     for c in range(CHUNKS):
         a, b = CHUNK * c, CHUNK * (c + 1)
@@ -140,14 +183,10 @@ def tile_ssm_channel_softplus_g2_kernel(tc, h, w_in, b_in, out_0, out_1, out_2):
         bias = sb.tile([P, GROUPS, PACK], F32, name="bias")
         nc.scalar.dma_start(out=bias_bf[:], in_=b_in.rearrange("(g p t) -> p g t", p=P, t=PACK))
 
-        zero = sb.tile([P, 1], F32, name="zero")
-        exp_zero = sb.tile([P, 1], F32, name="exp_zero")
-        nc.vector.memset(zero[:], 0.0)
-        nc.scalar.activation(out=exp_zero[:], in_=zero[:], func=ACT.Exp)
-
-        ones = sb.tile([P, HALF * PACK], BF16, name="ones", align_bytes=64)
-        ones_codes = sb.tile([P, HALF], U32, name="ones_codes", align_bytes=64)
-        ones_scales = sb.tile([P, HALF], U8, name="ones_scales", align_bytes=64)
+        exp_one = sb.tile([P, 1], F32, name="exp_one")
+        ones = sb.tile([P, P * PACK], BF16, name="ones", align_bytes=64)
+        ones_codes = sb.tile([P, P], U32, name="ones_codes", align_bytes=64)
+        ones_scales = sb.tile([P, P], U8, name="ones_scales", align_bytes=64)
 
         ident = sb.tile([P, P], F32, name="ident")
         make_identity(nc, ident[:])
@@ -159,7 +198,6 @@ def tile_ssm_channel_softplus_g2_kernel(tc, h, w_in, b_in, out_0, out_1, out_2):
         w_scales = sb.tile([P, GROUPS * PACK, PASSES, P], U8, name="w_scales", align_bytes=64)
 
         words_hbm = out_1.rearrange("g p m t -> g p (m t)").bitcast(I32)
-        scales_hbm = out_2.bitcast(I32)
 
         raw, shuf, turned, grouped, acc, y, y_bf, y_words, y_scales = {}, {}, {}, {}, {}, {}, {}, {}, {}
         fills = []
@@ -170,71 +208,68 @@ def tile_ssm_channel_softplus_g2_kernel(tc, h, w_in, b_in, out_0, out_1, out_2):
             fills.append(tag)
             return ps.tile([P, CHUNK], F32, name=tag, tag=tag)
 
-        def load(p):
-            kind, i = PAIRS[p]
-            tag = "raw%d" % (p % RAW_BUFS)
-            raw[p] = sb.tile([P, 2, D], BF16, name=tag, tag=tag)
+        def load(p, n):
+            kind, i = BLOCKS[p]
+            if p % 2 == 0:
+                tag = "raw%d" % (p % RAW_BUFS)
+                raw[p // 2] = sb.tile([P, 2, D], BF16, name=tag, tag=tag)
             if kind == "h":
-                src = h[2 * P * i : 2 * P * (i + 1), :].rearrange("(m s) k -> m s k", s=2)
+                src = h[P * i : P * (i + n), :].rearrange("(s m) k -> m s k", s=n)
             else:
-                rows = w_in[GROUP * (i // 2) : GROUP * (i // 2 + 1), :].rearrange("(m t) k -> m t k", t=PACK)
-                src = rows[:, 2 * (i % 2) : 2 * (i % 2) + 2, :]
-            nc.sync.dma_start(out=raw[p][:], in_=src)
+                g, t = i // PACK, i % PACK
+                rows = w_in[GROUP * g : GROUP * (g + 1), :].rearrange("(m t) k -> m t k", t=PACK)
+                src = rows[:, t : t + n, :]
+            nc.sync.dma_start(out=raw[p // 2][:, p % 2 : p % 2 + n, :], in_=src)
 
-        def shuffle(p):
+        def shuffle(p, engine):
             tag = "shuf%d" % (p % SHUF_BUFS)
-            shuf[p] = sb.tile([P, 2, 2 * D // 32, 16], BF16, name=tag, tag=tag)
-            nc.vector.tensor_copy(out=shuf[p][:], in_=raw[p][:].rearrange("p s (j u i) -> p u (s j) i", u=2, i=16))
+            shuf[p] = sb.tile([P, 2, D // 32, 16], BF16, name=tag, tag=tag)
+            nc.vector.tensor_copy(out=shuf[p][:], in_=raw[p // 2][:, p % 2, :].rearrange("p (j u i) -> p u j i", u=2, i=16))
 
-        def turn(p, b):
-            kind, i = PAIRS[p]
+        def turn(p):
             words = shuf[p][:].rearrange("p u j i -> p (u j i)").bitcast(F32)
             bank = next_bank()
-            turned[(p, b)] = bank
-            for o in range(2):
-                s, g = (o, b) if kind == "h" else (b, o)
-                for u in range(2):
-                    first = (u * 4 + s * 2 + g) * P
-                    col = (o * 2 + u) * P
-                    nc.tensor.transpose(bank[:, col : col + P], words[:, first : first + P], ident[:])
+            turned[p] = bank
+            for q in range(2 * PASSES):
+                nc.tensor.transpose(bank[:, P * q : P * (q + 1)], words[:, P * q : P * (q + 1)], ident[:])
 
-        def evac(p, b, engine):
-            kind, i = PAIRS[p]
-            tag = "grouped%d" % ((2 * p + b) % GROUPED_BUFS)
-            tile = sb.tile([P, 2 * P * PACK], BF16, name=tag, tag=tag, align_bytes=64)
-            grouped[(p, b)] = tile
-            if kind == "h":
-                src = turned[(p, b)][:].rearrange("p (q m) -> p m q", m=P)
-                dst = tile[:].bitcast(F32).rearrange("p (m q) -> p m q", m=P)
-            else:
-                src = turned[(p, b)][:].rearrange("p (g u m) -> p g m u", u=2, m=P)
-                dst = tile[:].bitcast(F32).rearrange("p (g m u) -> p g m u", u=2, m=P)
+        def evac(p, engine):
+            tag = "grouped%d" % (p % GROUPED_BUFS)
+            grouped[p] = sb.tile([P, PASSES, P * PACK], BF16, name=tag, tag=tag, align_bytes=64)
+            src = turned[p][:].rearrange("p (u k m) -> p k m u", u=2, m=P)
+            dst = grouped[p][:].bitcast(F32).rearrange("p k (m u) -> p k m u", u=2)
             if engine == "A":
                 nc.scalar.copy(out=dst, in_=src)
             else:
                 nc.vector.tensor_copy(out=dst, in_=src)
 
-        def quant(p, b):
-            kind, i = PAIRS[p]
+        def quant(p):
+            kind, i = BLOCKS[p]
             if kind == "h":
-                cols = slice(2 * P * i, 2 * P * (i + 1))
-                codes, scales = h_codes[:, b, cols], h_scales[:, b, cols]
+                cols = slice(P * i, P * (i + 1))
+                for k in range(PASSES):
+                    nc.vector.quantize_mx(
+                        out=h_codes[:, k, cols].bitcast(FP8X4), scales=h_scales[:, k, cols], in_=grouped[p][:, k, :]
+                    )
             else:
-                codes = w_codes[:, 2 * i + b, :, :].rearrange("p g m -> p (g m)")
-                scales = w_scales[:, 2 * i + b, :, :].rearrange("p g m -> p (g m)")
-            nc.vector.quantize_mx(out=codes.bitcast(FP8X4), scales=scales, in_=grouped[(p, b)][:])
+                nc.vector.quantize_mx(
+                    out=w_codes[:, i, :, :].rearrange("p k m -> p (k m)").bitcast(FP8X4),
+                    scales=w_scales[:, i, :, :].rearrange("p k m -> p (k m)"),
+                    in_=grouped[p][:].rearrange("p k c -> p (k c)"),
+                )
 
         def warm_prep():
-            nc.vector.memset(ones[:], 1.0)
+            nc.vector.memset(ones[:].bitcast(F32), 1.0)
+            nc.scalar.activation(out=exp_one[:], in_=ones[:].bitcast(F32)[:, 0:1], func=ACT.Exp)
             nc.vector.quantize_mx(out=ones_codes[:].bitcast(FP8X4), scales=ones_scales[:], in_=ones[:])
 
         def warm(p, n):
             bank = next_bank()
-            for i in range(2 * n):
+            for i in range(n):
                 nc.tensor.matmul_mx(
-                    out=bank[:, 0:HALF],
-                    lhsT=ones_codes[:, 0:P].bitcast(FP8X4),
-                    lhsT_scale=ones_scales[:, 0:P],
+                    out=bank[:, 0:P],
+                    lhsT=ones_codes[:].bitcast(FP8X4),
+                    lhsT_scale=ones_scales[:],
                     rhs=ones_codes[:].bitcast(FP8X4),
                     rhs_scale=ones_scales[:],
                     start=True,
@@ -299,10 +334,10 @@ def tile_ssm_channel_softplus_g2_kernel(tc, h, w_in, b_in, out_0, out_1, out_2):
             nc.sync.dma_start(out=words_hbm[g, :, a:b], in_=y_words[g][:, a:b].bitcast(I32))
 
         def store_scales(g, a, b, engine="Q"):
-            queue = nc.scalar if engine == "A" else nc.sync
+            queue = nc.sync
             for q in range(4):
                 queue.dma_start(
-                    out=scales_hbm[g, 4 * q : 4 * q + 4, a // 4 : b // 4],
+                    out=out_2[g, 4 * q : 4 * q + 4, a:b].bitcast(I32),
                     in_=y_scales[g][32 * q : 32 * q + 4, a:b].bitcast(I32),
                 )
 

@@ -23,153 +23,114 @@ GROUP = P * PACK
 GROUPS = E // GROUP
 BANKS = 8
 
-RAW_BUFS = 20
 SHUF_BUFS = 6
 GROUPED_BUFS = 4
 Y_BUFS = 3
+PIECES = [[0, 768, T], [0, T], [0, T], [0, CHUNK, 2 * CHUNK, T]]
+Y_TAGS = {(3, 0): "y0_0", (3, CHUNK): "y0_768"}
 YBF_BUFS = 3
-
-SHUFFLE = True
-PHASES = [("hhww" * 6, "wwww"), ("", "")]
-ORDER = "".join(x + y for x, y in PHASES)
-BLOCKS = [(c, ORDER[:i].count(c)) for i, c in enumerate(ORDER)]
-FIRST_BLOCKS = 24
-PLANES_AT = -1
-SINGLE_LOADS = 4
 WARM_UP = 16
-WARM_AFTER = [0, 0, 4, 4] + [0] * 20
-TILES_AFTER = [0, 0, 0, 0, 0, 0, 4, 0, 0, 8, 0, 0, 12, 0, 0, 12, 0, 0, 16, 0, 0, 16, 0, 0]
-LAG = 3
-AHEAD = 2
-QUANT_LAG = 1
-EVAC = list("AVAAAAAAAAAVAVAAVAVAVVAVVVVV")
+
+ORDER = "hhwwhhwwhhhhwwhhhhwwwwwwwwww"
+BLOCKS = [(c, ORDER[:i].count(c)) for i, c in enumerate(ORDER)]
+LOADS = [1,1,1,1,2,2,2,2,2,2,2,2,2,2,2,2]
+EVAC = "VAAAAAAAAVVVVVVVVVVVVVVVVVVV"
+SHUFFLE = "ssssssssssssssssssssssssssss"
+PHASES = ((((0,0,256,),(1,0,256,),(0,256,512,),(1,256,512,),(2,0,512,),(3,0,512,),(0,512,768,),(1,512,768,),(2,512,768,),(3,512,768,),),(("ln",0,0,1,0,768,),("ln",0,1,2,0,768,),("ln",0,2,3,0,768,),("ln",0,3,4,0,768,),("cast",0,0,512,),("cast",0,512,768,),("store_words",0,0,768,),),),(((0,768,1024,),(1,768,1024,),(2,768,1024,),(3,768,1024,),(4,0,512,),(4,512,1024,),(5,0,512,),(5,512,1024,),(0,1024,1536,),(1,1024,1536,),(2,1024,1536,),(3,1024,1536,),(4,1024,1536,),(5,1024,1536,),(6,0,512,),(6,512,1024,),(6,1024,1536,),(7,0,512,),(7,512,1024,),(7,1024,1536,),(8,0,512,),(8,512,1024,),(8,1024,1536,),(9,0,512,),(9,512,1024,),(9,1024,1536,),(10,0,512,),(10,512,1024,),(10,1024,1536,),(11,0,512,),(11,512,1024,),(11,1024,1536,),),(("ln",0,0,1,768,1536,),("ln",0,1,2,768,1536,),("ln",0,2,3,768,1536,),("ln",0,3,4,768,1536,),("cast",0,768,1024,),("cast",0,1024,1536,),("store_words",0,768,1536,),("store_scales",0,1,),("ln",1,0,1,0,1536,),("ln",1,1,2,0,1536,),("ln",1,2,3,0,1536,),("ln",1,3,4,0,1536,),("cast",1,0,512,),("cast",1,512,1024,),("cast",1,1024,1536,),("store_words",1,0,1536,),("store_scales",1,2,),("ln",2,0,1,0,1536,),("ln",2,1,2,0,1536,),("ln",2,2,3,0,1536,),("ln",2,3,4,0,1536,),("cast",2,0,512,),("cast",2,512,1024,),("cast",2,1024,1536,),("store_words",2,0,1536,),("store_scales",2,3,),),),(((12,0,512,),(12,512,1024,),(12,1024,1536,),(13,0,512,),(13,512,1024,),(13,1024,1536,),(14,0,512,),(14,512,1024,),(14,1024,1536,),(15,0,512,),(15,512,1024,),(15,1024,1536,),),(("ln",3,0,1,0,512,),("ln",3,1,2,0,512,),("ln",3,2,3,0,512,),("ln",3,3,4,0,512,),("cast",3,0,512,),("store_words",3,0,512,),("ln",3,0,2,512,1024,),("ln",3,2,4,512,1024,),("cast",3,512,1024,),("store_words",3,512,1024,),("ln",3,0,2,1024,1536,),("ln",3,2,4,1024,1536,),("cast",3,1024,1280,),("cast",3,1280,1536,),("store_words",3,1024,1536,),("store_scales",3,4,),),),)
+QUEUES = {
+    "Q": "LLLLLLLLLLLLLLLLYYYYWYYYYYYYYWYYYYWSSWSYYYYYYWYYWWS",
+    "P": "wttttttmttttmmmmmmmmmttttttttmmmmmmmmttttmmmmmmmmmmmmmmmttmmmmmmmmmttttmmmmmmmmmmmm",
+    "A": "eeeeexeeexxxxxxxxxllllxxxxxxxxxxxxxxxxxxxxxxxxxxxxxxxxllllllllllllxxxxxxxxxxxxllllllll",
+    "V": "psssesqqssqqssssqqqeqqqsssssseeesqqseeeqqessessqqqqsseeeeqqcqqeqceyqysssseeqeqeqqccyyccycyyccycyycycyccyy",
+}
+LETTER = {"turn": "t", "mm": "m", "warm": "w", "exp": "x", "ln": "l", "evac": "e", "shuffle": "s", "quant": "q",
+          "cast": "c", "quant_y": "y", "warm_prep": "p", "load": "L", "store_y": "Y", "store_words": "W",
+          "store_scales": "S"}
+
+
+def steps_and_needs():
+    steps, needs = [], {}
+
+    def add(step, before):
+        steps.append(step)
+        needs[step] = list(before)
+
+    loaded = {}
+    p = 0
+    for n in LOADS:
+        add(("load", p, n), [])
+        for x in range(p, p + n):
+            loaded[x] = ("load", p, n)
+        p += n
+    add(("warm_prep",), [])
+    add(("warm",), [("warm_prep",)])
+    shuffled = []
+    for p in range(len(BLOCKS)):
+        if SHUFFLE[p] == "s":
+            add(("shuffle", p), [loaded[p]] + [("turn", q) for q in shuffled[-SHUF_BUFS:-SHUF_BUFS + 1]if len(shuffled) >= SHUF_BUFS])
+            shuffled.append(p)
+        add(("turn", p), [("shuffle", p) if SHUFFLE[p] == "s" else loaded[p]])
+        add(("evac", p), [("turn", p)] + [("quant", q) for q in range(p - GROUPED_BUFS + 1)])
+        add(("quant", p), [("evac", p)])
+    for products, rest in PHASES:
+        for w, a, b in products:
+            add(("mm", w, a, b), [("quant", BLOCKS.index(("w", w)))] + [("quant", BLOCKS.index(("h", i))) for i in range(a // P, b // P)])
+            old = w // PACK - Y_BUFS
+            add(("exp", w, a, b), [("mm", w, a, b)] + [s for s in steps if s[0] in ("store_y", "cast") and s[1] == old])
+        for s in rest:
+            if s[0] == "ln":
+                g, t0, t1, a, b = s[1:]
+                add(s, [x for x in steps if x[0] == "exp" and PACK * g + t0 <= x[1] < PACK * g + t1 and x[2] < b and x[3] > a])
+                add(("store_y",) + s[1:], [s])
+            elif s[0] == "cast":
+                g, a, b = s[1:]
+                earlier = [x for x in steps if x[0] == "quant_y"]
+                add(s, [x for x in steps if x[0] == "ln" and x[1] == g and x[4] < b and x[5] > a] + earlier[: max(0, len(earlier) - YBF_BUFS + 1)])
+                add(("quant_y", g, a, b), [s])
+            elif s[0] == "store_words":
+                g, a, b = s[1:]
+                add(s, [x for x in steps if x[0] == "quant_y" and x[1] == g and x[2] < b and x[3] > a])
+            else:
+                add(s, [x for x in steps if x[0] == "quant_y" and x[1] == s[1]])
+    return steps, needs
+
+
+def engine_of(step):
+    if step[0] == "evac":
+        return EVAC[step[1]]
+    for engine, letters in (("Q", "LYWS"), ("P", "tmw"), ("A", "xl")):
+        if LETTER[step[0]] in letters:
+            return engine
+    return "V"
 
 
 def schedule():
-    steps = []
-    h_at = [BLOCKS.index(("h", i)) for i in range(T // P)]
-    w_at = [BLOCKS.index(("w", i)) for i in range(E // P)]
-    todo = [(w, i) for w in range(E // P) for i in range(T // P)]
-    todo.sort(key=lambda x: (max(w_at[x[0]], h_at[x[1]]), x))
-
-    def load(p):
-        if p < SINGLE_LOADS:
-            steps.append(("load", p, 1))
-        elif p % 2 == 0 and p < len(BLOCKS):
-            steps.append(("load", p, 2))
-
-    def shuffle(p):
-        if SHUFFLE and p < len(BLOCKS):
-            steps.append(("shuffle", p, "V"))
-
-    def prepare(p):
-        steps.append(("turn", p))
-        shuffle(p + AHEAD)
-        load(p + RAW_BUFS - 1)
-        steps.append(("evac", p, EVAC[p]))
-        quant(p - QUANT_LAG)
-
-    def quant(p):
-        if p >= 0 and ("quant", p) not in steps:
-            steps.append(("quant", p))
-
-    def multiply(tiles, newest):
-        while tiles > 0:
-            ready = [x for x in todo if max(w_at[x[0]], h_at[x[1]]) <= newest]
-            for n in (4, 2, 1):
-                runs = [x for x in ready if x[1] % n == 0 and all((x[0], x[1] + j) in ready for j in range(n))]
-                if runs:
-                    break
-            w, i = runs[0]
-            for j in range(n):
-                todo.remove((w, i + j))
-            steps.append(("mm", w // PACK, w % PACK, P * i, P * (i + n)))
-            steps.append(("exp", w // PACK, w % PACK, P * i, P * (i + n)))
-            tiles -= n
-
-    def planes(g, cuts):
-        for i in range(len(cuts) - 1):
-            steps.append(("cast", g, cuts[i], cuts[i + 1]))
-            if i > 0:
-                steps.append(("quant_y", g, cuts[i - 1], cuts[i]))
-        steps.append(("quant_y", g, cuts[-2], cuts[-1]))
-
-    for p in range(RAW_BUFS - 1):
-        load(p)
-    steps.append(("warm_prep",))
-    steps.append(("warm", -1, WARM_UP))
-    for p in range(AHEAD):
-        shuffle(p)
-    last = GROUPS - 1
-    logged = [0] * (E // P)
-    planed = [0] * GROUPS
-    stored = [0] * GROUPS
-
-    def make_planes():
-        for g in range(GROUPS):
-            upto = min(logged[PACK * g : PACK * (g + 1)])
-            if upto > planed[g]:
-                planes(g, list(range(planed[g], upto + 1, CHUNK)))
-                planed[g] = upto
-
-    def store_planes():
-        for g in range(GROUPS):
-            if planed[g] > stored[g]:
-                steps.append(("store_words", g, stored[g], planed[g]))
-                stored[g] = planed[g]
-                if planed[g] == T:
-                    steps.append(("store_scales", g, 0, T))
-
-    p = 0
-    for phase, (with_exp, with_ln) in enumerate(PHASES):
-        for kind in with_exp:
-            prepare(p)
-            if WARM_AFTER[p]:
-                steps.append(("warm", p, WARM_AFTER[p]))
-            multiply(TILES_AFTER[p], p - LAG)
-            if p == PLANES_AT:
-                quant(p)
-                make_planes()
-                store_planes()
-            p += 1
-        for q in range(p):
-            quant(q)
-        seen = ORDER[:p]
-        multiply(len([x for x in todo if x[0] < seen.count("w") and x[1] < seen.count("h")]), p - 1)
-        if phase == len(PHASES) - 1:
-            break
-        for kind in with_ln:
-            prepare(p)
-            p += 1
-        for q in range(p):
-            quant(q)
-        upto = P * seen.count("h")
-        first = True
-        for w in range(seen.count("w")):
-            g, t, a = w // PACK, w % PACK, logged[w]
-            for a, b in ([(a, a + CHUNK), (a + CHUNK, upto)] if first and upto > a + CHUNK else [(a, upto)]):
-                steps.append(("ln", g, t, t + 1, a, b))
-                steps.append(("store_y", g, t, t + 1, a, b))
-            first = False
-            logged[w] = upto
-            if t == PACK - 1 and phase == len(PHASES) - 2:
-                store_planes()
-                make_planes()
-        if phase == len(PHASES) - 2:
-            store_planes()
-
-    for c in range(CHUNKS):
-        a, b = CHUNK * c, CHUNK * (c + 1)
-        for t0, t1 in ([(0, 1), (1, 2), (2, 4)] if c == 0 else [(0, 2), (2, 4)]):
-            steps.append(("ln", last, t0, t1, a, b))
-            steps.append(("store_y", last, t0, t1, a, b))
-        steps.append(("cast", last, a, b))
-        steps.append(("quant_y", last, a, b))
-        if c > 0:
-            steps.append(("store_words", last, a - CHUNK, a))
-    steps.append(("store_words", last, T - CHUNK, T))
-    steps.append(("store_scales", last, 0, T, "A"))
-    return steps
+    steps, needs = steps_and_needs()
+    queues = {}
+    for engine, letters in QUEUES.items():
+        mine = [s for s in steps if engine_of(s) == engine]
+        queue = []
+        for letter in letters:
+            step = [s for s in mine if LETTER[s[0]] == letter][0]
+            mine.remove(step)
+            queue.append(step)
+        assert not mine
+        queues[engine] = queue
+    fills = queues["P"]
+    for i in range(BANKS, len(fills)):
+        old = fills[i - BANKS]
+        if old[0] != "warm":
+            needs[fills[i]].append((("evac" if old[0] == "turn" else "exp"),) + old[1:])
+    order, done = [], set()
+    while len(order) < len(steps):
+        count = len(order)
+        for engine in queues:
+            while queues[engine] and all(x in done for x in needs[queues[engine][0]]):
+                order.append(queues[engine][0])
+                done.add(queues[engine][0])
+                queues[engine] = queues[engine][1:]
+        assert len(order) > count
+    return order
 
 
 def tile_ssm_channel_softplus_g2_kernel(tc, h, w_in, b_in, out_0, out_1, out_2):
@@ -211,7 +172,7 @@ def tile_ssm_channel_softplus_g2_kernel(tc, h, w_in, b_in, out_0, out_1, out_2):
         def load(p, n):
             kind, i = BLOCKS[p]
             if p % 2 == 0:
-                tag = "raw%d" % (p % RAW_BUFS)
+                tag = "raw%d" % p
                 raw[p // 2] = sb.tile([P, 2, D], BF16, name=tag, tag=tag)
             if kind == "h":
                 src = h[P * i : P * (i + n), :].rearrange("(s m) k -> m s k", s=n)
@@ -221,24 +182,29 @@ def tile_ssm_channel_softplus_g2_kernel(tc, h, w_in, b_in, out_0, out_1, out_2):
                 src = rows[:, t : t + n, :]
             nc.sync.dma_start(out=raw[p // 2][:, p % 2 : p % 2 + n, :], in_=src)
 
-        def shuffle(p, engine):
-            tag = "shuf%d" % (p % SHUF_BUFS)
+        def shuffle(p):
+            tag = "shuf%d" % (len(shuf) % SHUF_BUFS)
             shuf[p] = sb.tile([P, 2, D // 32, 16], BF16, name=tag, tag=tag)
             nc.vector.tensor_copy(out=shuf[p][:], in_=raw[p // 2][:, p % 2, :].rearrange("p (j u i) -> p u j i", u=2, i=16))
 
         def turn(p):
-            words = shuf[p][:].rearrange("p u j i -> p (u j i)").bitcast(F32)
             bank = next_bank()
             turned[p] = bank
-            for q in range(2 * PASSES):
-                nc.tensor.transpose(bank[:, P * q : P * (q + 1)], words[:, P * q : P * (q + 1)], ident[:])
+            for u in range(2):
+                for k in range(PASSES):
+                    q = PASSES * u + k
+                    if p in shuf:
+                        words = shuf[p][:].rearrange("p u j i -> p (u j i)").bitcast(F32)[:, P * q : P * (q + 1)]
+                    else:
+                        words = raw[p // 2][:, p % 2, :].bitcast(F32)[:, 2 * P * k + u : 2 * P * (k + 1) : 2]
+                    nc.tensor.transpose(bank[:, P * q : P * (q + 1)], words, ident[:])
 
-        def evac(p, engine):
+        def evac(p):
             tag = "grouped%d" % (p % GROUPED_BUFS)
             grouped[p] = sb.tile([P, PASSES, P * PACK], BF16, name=tag, tag=tag, align_bytes=64)
             src = turned[p][:].rearrange("p (u k m) -> p k m u", u=2, m=P)
             dst = grouped[p][:].bitcast(F32).rearrange("p k (m u) -> p k m u", u=2)
-            if engine == "A":
+            if EVAC[p] == "A":
                 nc.scalar.copy(out=dst, in_=src)
             else:
                 nc.vector.tensor_copy(out=dst, in_=src)
@@ -263,9 +229,9 @@ def tile_ssm_channel_softplus_g2_kernel(tc, h, w_in, b_in, out_0, out_1, out_2):
             nc.scalar.activation(out=exp_one[:], in_=ones[:].bitcast(F32)[:, 0:1], func=ACT.Exp)
             nc.vector.quantize_mx(out=ones_codes[:].bitcast(FP8X4), scales=ones_scales[:], in_=ones[:])
 
-        def warm(p, n):
+        def warm():
             bank = next_bank()
-            for i in range(n):
+            for i in range(WARM_UP):
                 nc.tensor.matmul_mx(
                     out=bank[:, 0:P],
                     lhsT=ones_codes[:].bitcast(FP8X4),
@@ -276,7 +242,8 @@ def tile_ssm_channel_softplus_g2_kernel(tc, h, w_in, b_in, out_0, out_1, out_2):
                     stop=True,
                 )
 
-        def mm(g, t, a, b):
+        def mm(w, a, b):
+            g, t = w // PACK, w % PACK
             bank = next_bank()
             acc[(g, t, a)] = bank
             cols = slice(a, b)
@@ -291,24 +258,30 @@ def tile_ssm_channel_softplus_g2_kernel(tc, h, w_in, b_in, out_0, out_1, out_2):
                     stop=(k == PASSES - 1),
                 )
 
-        def exp(g, t, a, b):
-            if g not in y:
-                tag = "y%d" % (g % Y_BUFS)
-                y[g] = sb.tile([P, PACK, T], F32, name=tag, tag=tag)
+        def y_part(g, t0, t1, a, b):
+            i = max(j for j, x in enumerate(PIECES[g]) if x <= a)
+            lo, hi = PIECES[g][i], PIECES[g][i + 1]
+            if (g, lo) not in y:
+                tag = Y_TAGS.get((g, lo), "y%d_%d" % (g, lo))
+                y[(g, lo)] = sb.tile([P, PACK, hi - lo], F32, name=tag, tag=tag)
+            return y[(g, lo)][:, t0:t1, a - lo : b - lo]
+
+        def exp(w, a, b):
+            g, t = w // PACK, w % PACK
             nc.scalar.activation(
-                out=y[g][:, t, a:b],
+                out=y_part(g, t, t + 1, a, b).rearrange("p t m -> p (t m)"),
                 in_=acc[(g, t, a)][:, 0 : b - a],
                 func=ACT.Exp,
                 bias=bias[:, g, t : t + 1],
             )
 
         def ln(g, t0, t1, a, b):
-            part = y[g][:, t0:t1, a:b]
+            part = y_part(g, t0, t1, a, b)
             nc.scalar.activation(out=part, in_=part, func=ACT.Ln, bias=1.0)
 
         def store_y(g, t0, t1, a, b):
             rows = out_0[GROUP * g : GROUP * (g + 1), :].rearrange("(p t) m -> p t m", t=PACK)
-            nc.sync.dma_start(out=rows[:, t0:t1, a:b], in_=y[g][:, t0:t1, a:b])
+            nc.sync.dma_start(out=rows[:, t0:t1, a:b], in_=y_part(g, t0, t1, a, b))
 
         def cast(g, a, b):
             tag = "y_bf%d" % (len(casts) % YBF_BUFS)
@@ -317,7 +290,7 @@ def tile_ssm_channel_softplus_g2_kernel(tc, h, w_in, b_in, out_0, out_1, out_2):
             y_bf[(g, a)] = tile
             nc.vector.tensor_copy(
                 out=tile[:, 0 : (b - a) * PACK].rearrange("p (c i t) -> p c t i", i=4, t=PACK),
-                in_=y[g][:, :, a:b].rearrange("p t (c i) -> p c t i", i=4),
+                in_=y_part(g, 0, PACK, a, b).rearrange("p t (c i) -> p c t i", i=4),
             )
 
         def quant_y(g, a, b):
@@ -333,10 +306,10 @@ def tile_ssm_channel_softplus_g2_kernel(tc, h, w_in, b_in, out_0, out_1, out_2):
         def store_words(g, a, b):
             nc.sync.dma_start(out=words_hbm[g, :, a:b], in_=y_words[g][:, a:b].bitcast(I32))
 
-        def store_scales(g, a, b, engine="Q"):
-            queue = nc.sync
+        def store_scales(g, g1):
+            a, b = 0, T
             for q in range(4):
-                queue.dma_start(
+                nc.sync.dma_start(
                     out=out_2[g, 4 * q : 4 * q + 4, a:b].bitcast(I32),
                     in_=y_scales[g][32 * q : 32 * q + 4, a:b].bitcast(I32),
                 )

@@ -16,36 +16,75 @@ ACT = mybir.ActivationFunctionType
 
 P = 128
 PACK = 4
-PASSES = 2
+PASSES = D // (P * PACK)
 CHUNK = 512
-CHUNKS = T // CHUNK
+HALF = CHUNK // 2
 GROUP = P * PACK
 GROUPS = E // GROUP
+LAST = GROUPS - 1
 BANKS = 8
+QUADRANT = 32
+SCALE_ROWS = 4
 
-SHUF_BUFS = 6
-GROUPED_BUFS = 4
-Y_BUFS = 3
-PIECES = [[0, 768, T], [0, T], [0, T], [0, CHUNK, 2 * CHUNK, T]]
-Y_TAGS = {(3, 0): "y0_0", (3, CHUNK): "y0_768"}
-YBF_BUFS = 3
+SORTED_BUFS = 6
+TURNED_BUFS = 4
+Y_BF_BUFS = 3
 WARM_UP = 16
 
-ORDER = "hhwwhhwwhhhhwwhhhhwwwwwwwwww"
-BLOCKS = [(c, ORDER[:i].count(c)) for i, c in enumerate(ORDER)]
-LOADS = [1,1,1,1,2,2,2,2,2,2,2,2,2,2,2,2]
-EVAC = "VAAAAAAAAVVVVVVVVVVVVVVVVVVV"
-SHUFFLE = "ssssssssssssssssssssssssssss"
-PHASES = ((((0,0,256,),(1,0,256,),(0,256,512,),(1,256,512,),(2,0,512,),(3,0,512,),(0,512,768,),(1,512,768,),(2,512,768,),(3,512,768,),),(("ln",0,0,1,0,768,),("ln",0,1,2,0,768,),("ln",0,2,3,0,768,),("ln",0,3,4,0,768,),("cast",0,0,512,),("cast",0,512,768,),("store_words",0,0,768,),),),(((0,768,1024,),(1,768,1024,),(2,768,1024,),(3,768,1024,),(4,0,512,),(4,512,1024,),(5,0,512,),(5,512,1024,),(0,1024,1536,),(1,1024,1536,),(2,1024,1536,),(3,1024,1536,),(4,1024,1536,),(5,1024,1536,),(6,0,512,),(6,512,1024,),(6,1024,1536,),(7,0,512,),(7,512,1024,),(7,1024,1536,),(8,0,512,),(8,512,1024,),(8,1024,1536,),(9,0,512,),(9,512,1024,),(9,1024,1536,),(10,0,512,),(10,512,1024,),(10,1024,1536,),(11,0,512,),(11,512,1024,),(11,1024,1536,),),(("ln",0,0,1,768,1536,),("ln",0,1,2,768,1536,),("ln",0,2,3,768,1536,),("ln",0,3,4,768,1536,),("cast",0,768,1024,),("cast",0,1024,1536,),("store_words",0,768,1536,),("store_scales",0,1,),("ln",1,0,1,0,1536,),("ln",1,1,2,0,1536,),("ln",1,2,3,0,1536,),("ln",1,3,4,0,1536,),("cast",1,0,512,),("cast",1,512,1024,),("cast",1,1024,1536,),("store_words",1,0,1536,),("store_scales",1,2,),("ln",2,0,1,0,1536,),("ln",2,1,2,0,1536,),("ln",2,2,3,0,1536,),("ln",2,3,4,0,1536,),("cast",2,0,512,),("cast",2,512,1024,),("cast",2,1024,1536,),("store_words",2,0,1536,),("store_scales",2,3,),),),(((12,0,512,),(12,512,1024,),(12,1024,1536,),(13,0,512,),(13,512,1024,),(13,1024,1536,),(14,0,512,),(14,512,1024,),(14,1024,1536,),(15,0,512,),(15,512,1024,),(15,1024,1536,),),(("ln",3,0,1,0,512,),("ln",3,1,2,0,512,),("ln",3,2,3,0,512,),("ln",3,3,4,0,512,),("cast",3,0,512,),("store_words",3,0,512,),("ln",3,0,2,512,1024,),("ln",3,2,4,512,1024,),("cast",3,512,1024,),("store_words",3,512,1024,),("ln",3,0,2,1024,1536,),("ln",3,2,4,1024,1536,),("cast",3,1024,1280,),("cast",3,1280,1536,),("store_words",3,1024,1536,),("store_scales",3,4,),),),)
+ORDER = "hhwwhhwwhh" + "hhwwhhhh" + "w" * 10
+BLOCKS = [(kind, ORDER[:n].count(kind)) for n, kind in enumerate(ORDER)]
+SINGLE_LOADS = 4
+COPIER = "V" + "A" * 8 + "V" * 19
+EARLY = 768
+
+Y_CUTS = [[0, EARLY, T], [0, T], [0, T], [0, CHUNK, 2 * CHUNK, T]]
+Y_REUSE = {(LAST, 0): (0, 0), (LAST, CHUNK): (0, EARLY)}
+
+LETTER = {"turn": "t", "product": "m", "warm_up": "w", "copy_out": "e", "exp": "x", "ln": "l", "constant": "k",
+          "sort": "s", "quantise": "q", "cast": "c", "quantise_y": "y", "load": "L", "store_y": "Y",
+          "store_words": "W", "store_scales": "S"}
 QUEUES = {
-    "Q": "LLLLLLLLLLLLLLLLYYYYWYYYYYYYYWYYYYWSSWSYYYYYYWYYWWS",
-    "P": "wttttttmttttmmmmmmmmmttttttttmmmmmmmmttttmmmmmmmmmmmmmmmttmmmmmmmmmttttmmmmmmmmmmmm",
-    "A": "eeeeexeeexxxxxxxxxllllxxxxxxxxxxxxxxxxxxxxxxxxxxxxxxxxllllllllllllxxxxxxxxxxxxllllllll",
-    "V": "psssesqqssqqssssqqqeqqqsssssseeesqqseeeqqessessqqqqsseeeeqqcqqeqceyqysssseeqeqeqqccyyccycyyccycyycycyccyy",
+    "sync": "L" * 16 + "YYYYW" + "YYYY" + "YYYYW" + "YYYYWW" + "YYYY" + "YYW" + "YYWWS",
+    "tensor": "wttttttmttttmmmmmmmmm" + "t" * 8 + "m" * 8 + "tttt" + "m" * 15 + "tt" + "m" * 9 + "tttt" + "m" * 12,
+    "scalar": "eeeeexeeexxxxxxxxx|llll|" + "x" * 32 + "|" + "l" * 12 + "|" + "x" * 12 + "|" + "l" * 8,
+    "vector": "ksssesqqssqqssssqqqeqqq" + "sssssseeesqqseeeqqessessqqqqsseeeeqqcqqeqceyqy" + "sssseeqeqeqq"
+    + "ccyy" + "ccycyy" * 2 + "cy" * 2 + "ccyy",
 }
-LETTER = {"turn": "t", "mm": "m", "warm": "w", "exp": "x", "ln": "l", "evac": "e", "shuffle": "s", "quant": "q",
-          "cast": "c", "quant_y": "y", "warm_prep": "p", "load": "L", "store_y": "Y", "store_words": "W",
-          "store_scales": "S"}
+
+
+def chunks(weights):
+    return [(w, a, a + CHUNK) for w in weights for a in range(0, T, CHUNK)]
+
+
+def ln_rows(g, a, b):
+    return [("ln", g, t, t + 1, a, b) for t in range(PACK)]
+
+
+def planes(g, cuts):
+    return [("cast", g, a, b) for a, b in zip(cuts, cuts[1:])] + [("store_words", g, cuts[0], cuts[-1])]
+
+
+def phases():
+    first = range(PACK)
+    thirds = [0, CHUNK, 2 * CHUNK, T]
+    products_1 = [(w, a, a + HALF) for a in (0, HALF) for w in (0, 1)] + [(w, 0, CHUNK) for w in (2, 3)]
+    products_1 += [(w, CHUNK, EARLY) for w in first]
+    after_1 = ln_rows(0, 0, EARLY) + planes(0, [0, CHUNK, EARLY])
+    products_2 = [(w, EARLY, 2 * CHUNK) for w in first] + [(w, a, a + CHUNK) for w in (4, 5) for a in (0, CHUNK)]
+    products_2 += [(w, 2 * CHUNK, T) for w in range(6)] + chunks(range(6, PACK * LAST))
+    after_2 = ln_rows(0, EARLY, T) + planes(0, [EARLY, 2 * CHUNK, T])
+    for g in range(1, LAST):
+        after_2 += ln_rows(g, 0, T) + planes(g, thirds)
+    after_3 = ln_rows(LAST, 0, CHUNK) + planes(LAST, thirds[:2])
+    for cuts in (thirds[1:3], [2 * CHUNK, T - HALF, T]):
+        after_3 += [("ln", LAST, t, t + 2, cuts[0], cuts[-1]) for t in (0, 2)] + planes(LAST, cuts)
+    after_3 += [("store_scales",)]
+    return [(products_1, after_1), (products_2, after_2), (chunks(range(PACK * LAST, PACK * GROUPS)), after_3)]
+
+
+def y_piece(g, a):
+    n = max(j for j, cut in enumerate(Y_CUTS[g]) if cut <= a)
+    return Y_CUTS[g][n], Y_CUTS[g][n + 1]
 
 
 def steps_and_needs():
@@ -53,83 +92,76 @@ def steps_and_needs():
 
     def add(step, before):
         steps.append(step)
-        needs[step] = list(before)
+        needs[step] = before
 
-    loaded = {}
-    p = 0
-    for n in LOADS:
-        add(("load", p, n), [])
-        for x in range(p, p + n):
-            loaded[x] = ("load", p, n)
-        p += n
-    add(("warm_prep",), [])
-    add(("warm",), [("warm_prep",)])
-    shuffled = []
-    for p in range(len(BLOCKS)):
-        if SHUFFLE[p] == "s":
-            add(("shuffle", p), [loaded[p]] + [("turn", q) for q in shuffled[-SHUF_BUFS:-SHUF_BUFS + 1]if len(shuffled) >= SHUF_BUFS])
-            shuffled.append(p)
-        add(("turn", p), [("shuffle", p) if SHUFFLE[p] == "s" else loaded[p]])
-        add(("evac", p), [("turn", p)] + [("quant", q) for q in range(p - GROUPED_BUFS + 1)])
-        add(("quant", p), [("evac", p)])
-    for products, rest in PHASES:
+    def meeting(kind, g, a, b):
+        return [s for s in steps if s[0] == kind and s[1] == g and s[-2] < b and s[-1] > a]
+
+    for n in list(range(SINGLE_LOADS)) + list(range(SINGLE_LOADS, len(BLOCKS), 2)):
+        add(("load", n), [])
+    add(("constant",), [])
+    add(("warm_up",), [("constant",)])
+    for n in range(len(BLOCKS)):
+        load = ("load", n if n < SINGLE_LOADS else n - n % 2)
+        add(("sort", n), [load] + [("turn", j) for j in range(n - SORTED_BUFS + 1)])
+        add(("turn", n), [("sort", n)])
+        add(("copy_out", n), [("turn", n)] + [("quantise", j) for j in range(n - TURNED_BUFS + 1)])
+        add(("quantise", n), [("copy_out", n)])
+    for products, after in phases():
         for w, a, b in products:
-            add(("mm", w, a, b), [("quant", BLOCKS.index(("w", w)))] + [("quant", BLOCKS.index(("h", i))) for i in range(a // P, b // P)])
-            old = w // PACK - Y_BUFS
-            add(("exp", w, a, b), [("mm", w, a, b)] + [s for s in steps if s[0] in ("store_y", "cast") and s[1] == old])
-        for s in rest:
-            if s[0] == "ln":
-                g, t0, t1, a, b = s[1:]
-                add(s, [x for x in steps if x[0] == "exp" and PACK * g + t0 <= x[1] < PACK * g + t1 and x[2] < b and x[3] > a])
-                add(("store_y",) + s[1:], [s])
-            elif s[0] == "cast":
-                g, a, b = s[1:]
-                earlier = [x for x in steps if x[0] == "quant_y"]
-                add(s, [x for x in steps if x[0] == "ln" and x[1] == g and x[4] < b and x[5] > a] + earlier[: max(0, len(earlier) - YBF_BUFS + 1)])
-                add(("quant_y", g, a, b), [s])
-            elif s[0] == "store_words":
-                g, a, b = s[1:]
-                add(s, [x for x in steps if x[0] == "quant_y" and x[1] == g and x[2] < b and x[3] > a])
+            operands = [("w", w)] + [("h", j) for j in range(a // P, b // P)]
+            add(("product", w, a, b), [("quantise", BLOCKS.index(x)) for x in operands])
+            readers = []
+            if (w // PACK, a) in Y_REUSE:
+                g, start = Y_REUSE[(w // PACK, a)]
+                readers = meeting("store_y", g, *y_piece(g, start)) + meeting("cast", g, *y_piece(g, start))
+            add(("exp", w, a, b), [("product", w, a, b)] + readers)
+        for step in after:
+            kind = step[0]
+            if kind == "ln":
+                g, t0, t1, a, b = step[1:]
+                add(step, [s for t in range(t0, t1) for s in meeting("exp", PACK * g + t, a, b)])
+                add(("store_y",) + step[1:], [step])
+            elif kind == "cast":
+                earlier = [s for s in steps if s[0] == "quantise_y"]
+                add(step, meeting("ln", *step[1:]) + earlier[: max(0, len(earlier) - Y_BF_BUFS + 1)])
+                add(("quantise_y",) + step[1:], [step])
+            elif kind == "store_words":
+                add(step, meeting("quantise_y", *step[1:]))
             else:
-                add(s, [x for x in steps if x[0] == "quant_y" and x[1] == s[1]])
+                add(step, [s for s in steps if s[0] == "quantise_y"])
     return steps, needs
 
 
 def engine_of(step):
-    if step[0] == "evac":
-        return EVAC[step[1]]
-    for engine, letters in (("Q", "LYWS"), ("P", "tmw"), ("A", "xl")):
-        if LETTER[step[0]] in letters:
-            return engine
-    return "V"
+    if step[0] == "copy_out":
+        return "scalar" if COPIER[step[1]] == "A" else "vector"
+    return [engine for engine, letters in QUEUES.items() if LETTER[step[0]] in letters][0]
 
 
 def schedule():
     steps, needs = steps_and_needs()
     queues = {}
     for engine, letters in QUEUES.items():
-        mine = [s for s in steps if engine_of(s) == engine]
-        queue = []
-        for letter in letters:
-            step = [s for s in mine if LETTER[s[0]] == letter][0]
-            mine.remove(step)
-            queue.append(step)
-        assert not mine
-        queues[engine] = queue
-    fills = queues["P"]
-    for i in range(BANKS, len(fills)):
-        old = fills[i - BANKS]
-        if old[0] != "warm":
-            needs[fills[i]].append((("evac" if old[0] == "turn" else "exp"),) + old[1:])
-    order, done = [], set()
+        left = [s for s in steps if engine_of(s) == engine]
+        queues[engine] = []
+        for letter in letters.replace("|", ""):
+            step = [s for s in left if LETTER[s[0]] == letter][0]
+            left.remove(step)
+            queues[engine].append(step)
+        assert not left
+    fills = queues["tensor"]
+    for old, step in zip(fills, fills[BANKS:]):
+        if old[0] != "warm_up":
+            needs[step].append(("copy_out" if old[0] == "turn" else "exp",) + old[1:])
+    order = []
     while len(order) < len(steps):
-        count = len(order)
-        for engine in queues:
-            while queues[engine] and all(x in done for x in needs[queues[engine][0]]):
-                order.append(queues[engine][0])
-                done.add(queues[engine][0])
-                queues[engine] = queues[engine][1:]
-        assert len(order) > count
+        before = len(order)
+        for queue in queues.values():
+            while queue and all(s in order for s in needs[queue[0]]):
+                order.append(queue[0])
+                queue.remove(queue[0])
+        assert len(order) > before
     return order
 
 
@@ -144,133 +176,118 @@ def tile_ssm_channel_softplus_g2_kernel(tc, h, w_in, b_in, out_0, out_1, out_2):
         bias = sb.tile([P, GROUPS, PACK], F32, name="bias")
         nc.scalar.dma_start(out=bias_bf[:], in_=b_in.rearrange("(g p t) -> p g t", p=P, t=PACK))
 
-        exp_one = sb.tile([P, 1], F32, name="exp_one")
-        ones = sb.tile([P, P * PACK], BF16, name="ones", align_bytes=64)
-        ones_codes = sb.tile([P, P], U32, name="ones_codes", align_bytes=64)
-        ones_scales = sb.tile([P, P], U8, name="ones_scales", align_bytes=64)
-
         ident = sb.tile([P, P], F32, name="ident")
         make_identity(nc, ident[:])
         nc.gpsimd.tensor_copy(out=bias[:], in_=bias_bf[:])
+
+        const = sb.tile([P, P * PACK], BF16, name="const", align_bytes=64)
+        const_codes = sb.tile([P, P], U32, name="const_codes", align_bytes=64)
+        const_scales = sb.tile([P, P], U8, name="const_scales", align_bytes=64)
+        const_exp = sb.tile([P, 1], F32, name="const_exp")
 
         h_codes = sb.tile([P, PASSES, T], U32, name="h_codes", align_bytes=64)
         h_scales = sb.tile([P, PASSES, T], U8, name="h_scales", align_bytes=64)
         w_codes = sb.tile([P, GROUPS * PACK, PASSES, P], U32, name="w_codes", align_bytes=64)
         w_scales = sb.tile([P, GROUPS * PACK, PASSES, P], U8, name="w_scales", align_bytes=64)
+        y_words = [sb.tile([P, T], U32, name="y_words%d" % g, align_bytes=64) for g in range(GROUPS)]
+        y_scales = sb.tile([P, T], U8, name="y_scales", align_bytes=64)
 
-        words_hbm = out_1.rearrange("g p m t -> g p (m t)").bitcast(I32)
+        raw, ordered, turned, filled, y, y_bf = {}, {}, {}, {}, {}, {}
 
-        raw, shuf, turned, grouped, acc, y, y_bf, y_words, y_scales = {}, {}, {}, {}, {}, {}, {}, {}, {}
-        fills = []
-        casts = []
+        def next_bank(user):
+            filled[user] = ps.tile([P, CHUNK], F32, name="bank%d" % (len(filled) % BANKS))
+            return filled[user]
 
-        def next_bank():
-            tag = "bank%d" % (len(fills) % BANKS)
-            fills.append(tag)
-            return ps.tile([P, CHUNK], F32, name=tag, tag=tag)
+        def y_part(g, t0, t1, a, b):
+            start, end = y_piece(g, a)
+            if (g, start) not in y:
+                y[(g, start)] = sb.tile([P, PACK, end - start], F32, name="y%d_%d" % Y_REUSE.get((g, start), (g, start)))
+            return y[(g, start)][:, t0:t1, a - start : b - start]
 
-        def load(p, n):
-            kind, i = BLOCKS[p]
-            if p % 2 == 0:
-                tag = "raw%d" % p
-                raw[p // 2] = sb.tile([P, 2, D], BF16, name=tag, tag=tag)
+        def load(n):
+            kind, j = BLOCKS[n]
+            count = 1 if n < SINGLE_LOADS else 2
+            if n % 2 == 0:
+                raw[n // 2] = sb.tile([P, 2, D], BF16, name="raw%d" % n)
             if kind == "h":
-                src = h[P * i : P * (i + n), :].rearrange("(s m) k -> m s k", s=n)
+                rows = h[P * j : P * (j + count), :].rearrange("(s m) k -> m s k", s=count)
             else:
-                g, t = i // PACK, i % PACK
-                rows = w_in[GROUP * g : GROUP * (g + 1), :].rearrange("(m t) k -> m t k", t=PACK)
-                src = rows[:, t : t + n, :]
-            nc.sync.dma_start(out=raw[p // 2][:, p % 2 : p % 2 + n, :], in_=src)
+                g, t = j // PACK, j % PACK
+                rows = w_in[GROUP * g : GROUP * (g + 1), :].rearrange("(m t) k -> m t k", t=PACK)[:, t : t + count, :]
+            nc.sync.dma_start(out=raw[n // 2][:, n % 2 : n % 2 + count, :], in_=rows)
 
-        def shuffle(p):
-            tag = "shuf%d" % (len(shuf) % SHUF_BUFS)
-            shuf[p] = sb.tile([P, 2, D // 32, 16], BF16, name=tag, tag=tag)
-            nc.vector.tensor_copy(out=shuf[p][:], in_=raw[p // 2][:, p % 2, :].rearrange("p (j u i) -> p u j i", u=2, i=16))
+        def constant():
+            nc.vector.memset(const[:].bitcast(F32), 1.0)
+            nc.scalar.activation(out=const_exp[:], in_=const[:].bitcast(F32)[:, 0:1], func=ACT.Exp)
+            nc.vector.quantize_mx(out=const_codes[:].bitcast(FP8X4), scales=const_scales[:], in_=const[:])
 
-        def turn(p):
-            bank = next_bank()
-            turned[p] = bank
-            for u in range(2):
-                for k in range(PASSES):
-                    q = PASSES * u + k
-                    if p in shuf:
-                        words = shuf[p][:].rearrange("p u j i -> p (u j i)").bitcast(F32)[:, P * q : P * (q + 1)]
-                    else:
-                        words = raw[p // 2][:, p % 2, :].bitcast(F32)[:, 2 * P * k + u : 2 * P * (k + 1) : 2]
-                    nc.tensor.transpose(bank[:, P * q : P * (q + 1)], words, ident[:])
-
-        def evac(p):
-            tag = "grouped%d" % (p % GROUPED_BUFS)
-            grouped[p] = sb.tile([P, PASSES, P * PACK], BF16, name=tag, tag=tag, align_bytes=64)
-            src = turned[p][:].rearrange("p (u k m) -> p k m u", u=2, m=P)
-            dst = grouped[p][:].bitcast(F32).rearrange("p k (m u) -> p k m u", u=2)
-            if EVAC[p] == "A":
-                nc.scalar.copy(out=dst, in_=src)
-            else:
-                nc.vector.tensor_copy(out=dst, in_=src)
-
-        def quant(p):
-            kind, i = BLOCKS[p]
-            if kind == "h":
-                cols = slice(P * i, P * (i + 1))
-                for k in range(PASSES):
-                    nc.vector.quantize_mx(
-                        out=h_codes[:, k, cols].bitcast(FP8X4), scales=h_scales[:, k, cols], in_=grouped[p][:, k, :]
-                    )
-            else:
-                nc.vector.quantize_mx(
-                    out=w_codes[:, i, :, :].rearrange("p k m -> p (k m)").bitcast(FP8X4),
-                    scales=w_scales[:, i, :, :].rearrange("p k m -> p (k m)"),
-                    in_=grouped[p][:].rearrange("p k c -> p (k c)"),
-                )
-
-        def warm_prep():
-            nc.vector.memset(ones[:].bitcast(F32), 1.0)
-            nc.scalar.activation(out=exp_one[:], in_=ones[:].bitcast(F32)[:, 0:1], func=ACT.Exp)
-            nc.vector.quantize_mx(out=ones_codes[:].bitcast(FP8X4), scales=ones_scales[:], in_=ones[:])
-
-        def warm():
-            bank = next_bank()
-            for i in range(WARM_UP):
+        def warm_up():
+            bank = next_bank("warm_up")
+            for repeat in range(WARM_UP):
                 nc.tensor.matmul_mx(
                     out=bank[:, 0:P],
-                    lhsT=ones_codes[:].bitcast(FP8X4),
-                    lhsT_scale=ones_scales[:],
-                    rhs=ones_codes[:].bitcast(FP8X4),
-                    rhs_scale=ones_scales[:],
+                    lhsT=const_codes[:].bitcast(FP8X4),
+                    lhsT_scale=const_scales[:],
+                    rhs=const_codes[:].bitcast(FP8X4),
+                    rhs_scale=const_scales[:],
                     start=True,
                     stop=True,
                 )
 
-        def mm(w, a, b):
-            g, t = w // PACK, w % PACK
-            bank = next_bank()
-            acc[(g, t, a)] = bank
-            cols = slice(a, b)
-            for k in range(PASSES):
-                nc.tensor.matmul_mx(
-                    out=bank[:, 0 : b - a],
-                    lhsT=w_codes[:, PACK * g + t, k, :].bitcast(FP8X4),
-                    lhsT_scale=w_scales[:, PACK * g + t, k, :],
-                    rhs=h_codes[:, k, cols].bitcast(FP8X4),
-                    rhs_scale=h_scales[:, k, cols],
-                    start=(k == 0),
-                    stop=(k == PASSES - 1),
+        def sort(n):
+            ordered[n] = sb.tile([P, 2, D // 32, 16], BF16, name="ordered%d" % (n % SORTED_BUFS))
+            rows = raw[n // 2][:, n % 2, :]
+            nc.vector.tensor_copy(out=ordered[n][:], in_=rows.rearrange("p (j u r) -> p u j r", u=2, r=16))
+
+        def turn(n):
+            words = ordered[n][:].rearrange("p u j r -> p (u j r)").bitcast(F32)
+            bank = next_bank(n)
+            for quarter in range(2 * PASSES):
+                cols = slice(P * quarter, P * (quarter + 1))
+                nc.tensor.transpose(bank[:, cols], words[:, cols], ident[:])
+
+        def copy_out(n):
+            turned[n] = sb.tile([P, PASSES, P * PACK], BF16, name="turned%d" % (n % TURNED_BUFS), align_bytes=64)
+            src = filled[n][:].rearrange("p (u c m) -> p c m u", u=2, m=P)
+            dst = turned[n][:].bitcast(F32).rearrange("p c (m u) -> p c m u", u=2)
+            if COPIER[n] == "A":
+                nc.scalar.copy(out=dst, in_=src)
+            else:
+                nc.vector.tensor_copy(out=dst, in_=src)
+
+        def quantise(n):
+            kind, j = BLOCKS[n]
+            if kind == "h":
+                cols = slice(P * j, P * (j + 1))
+                for c in range(PASSES):
+                    nc.vector.quantize_mx(
+                        out=h_codes[:, c, cols].bitcast(FP8X4), scales=h_scales[:, c, cols], in_=turned[n][:, c, :]
+                    )
+            else:
+                nc.vector.quantize_mx(
+                    out=w_codes[:, j, :, :].rearrange("p c m -> p (c m)").bitcast(FP8X4),
+                    scales=w_scales[:, j, :, :].rearrange("p c m -> p (c m)"),
+                    in_=turned[n][:].rearrange("p c x -> p (c x)"),
                 )
 
-        def y_part(g, t0, t1, a, b):
-            i = max(j for j, x in enumerate(PIECES[g]) if x <= a)
-            lo, hi = PIECES[g][i], PIECES[g][i + 1]
-            if (g, lo) not in y:
-                tag = Y_TAGS.get((g, lo), "y%d_%d" % (g, lo))
-                y[(g, lo)] = sb.tile([P, PACK, hi - lo], F32, name=tag, tag=tag)
-            return y[(g, lo)][:, t0:t1, a - lo : b - lo]
+        def product(w, a, b):
+            bank = next_bank((w, a))
+            for c in range(PASSES):
+                nc.tensor.matmul_mx(
+                    out=bank[:, 0 : b - a],
+                    lhsT=w_codes[:, w, c, :].bitcast(FP8X4),
+                    lhsT_scale=w_scales[:, w, c, :],
+                    rhs=h_codes[:, c, a:b].bitcast(FP8X4),
+                    rhs_scale=h_scales[:, c, a:b],
+                    start=(c == 0),
+                    stop=(c == PASSES - 1),
+                )
 
         def exp(w, a, b):
             g, t = w // PACK, w % PACK
             nc.scalar.activation(
                 out=y_part(g, t, t + 1, a, b).rearrange("p t m -> p (t m)"),
-                in_=acc[(g, t, a)][:, 0 : b - a],
+                in_=filled[(w, a)][:, 0 : b - a],
                 func=ACT.Exp,
                 bias=bias[:, g, t : t + 1],
             )
@@ -284,38 +301,31 @@ def tile_ssm_channel_softplus_g2_kernel(tc, h, w_in, b_in, out_0, out_1, out_2):
             nc.sync.dma_start(out=rows[:, t0:t1, a:b], in_=y_part(g, t0, t1, a, b))
 
         def cast(g, a, b):
-            tag = "y_bf%d" % (len(casts) % YBF_BUFS)
-            casts.append(tag)
-            tile = sb.tile([P, CHUNK * PACK], BF16, name=tag, tag=tag, align_bytes=64)
-            y_bf[(g, a)] = tile
+            tile = sb.tile([P, CHUNK * PACK], BF16, name="y_bf%d" % (len(y_bf) % Y_BF_BUFS), align_bytes=64)
+            y_bf[(g, a)] = tile[:, 0 : (b - a) * PACK]
             nc.vector.tensor_copy(
-                out=tile[:, 0 : (b - a) * PACK].rearrange("p (c i t) -> p c t i", i=4, t=PACK),
-                in_=y_part(g, 0, PACK, a, b).rearrange("p t (c i) -> p c t i", i=4),
+                out=y_bf[(g, a)].rearrange("p (m r t) -> p m t r", r=4, t=PACK),
+                in_=y_part(g, 0, PACK, a, b).rearrange("p t (m r) -> p m t r", r=4),
             )
 
-        def quant_y(g, a, b):
-            if g not in y_words:
-                y_words[g] = sb.tile([P, T], U32, name="y_words%d" % g, align_bytes=64)
-                y_scales[g] = sb.tile([P, T], U8, name="y_scales%d" % g, align_bytes=64)
+        def quantise_y(g, a, b):
             nc.vector.quantize_mx(
-                out=y_words[g][:, a:b].bitcast(FP8X4),
-                scales=y_scales[g][:, a:b],
-                in_=y_bf[(g, a)][:, 0 : (b - a) * PACK],
+                out=y_words[g][:, a:b].bitcast(FP8X4), scales=y_scales[SCALE_ROWS * g :, a:b], in_=y_bf[(g, a)]
             )
 
         def store_words(g, a, b):
-            nc.sync.dma_start(out=words_hbm[g, :, a:b], in_=y_words[g][:, a:b].bitcast(I32))
+            words = out_1.rearrange("g p m t -> g p (m t)").bitcast(I32)
+            nc.sync.dma_start(out=words[g, :, a:b], in_=y_words[g][:, a:b].bitcast(I32))
 
-        def store_scales(g, g1):
-            a, b = 0, T
-            for q in range(4):
+        def store_scales():
+            for q in range(P // QUADRANT):
                 nc.sync.dma_start(
-                    out=out_2[g, 4 * q : 4 * q + 4, a:b].bitcast(I32),
-                    in_=y_scales[g][32 * q : 32 * q + 4, a:b].bitcast(I32),
+                    out=out_2[:, SCALE_ROWS * q : SCALE_ROWS * (q + 1), :].bitcast(I32),
+                    in_=y_scales[QUADRANT * q : QUADRANT * q + SCALE_ROWS * GROUPS, :].bitcast(I32),
                 )
 
-        emit = {"load": load, "shuffle": shuffle, "turn": turn, "evac": evac, "quant": quant, "mm": mm, "warm": warm, "warm_prep": warm_prep, "exp": exp,
-                "ln": ln, "store_y": store_y, "cast": cast, "quant_y": quant_y, "store_words": store_words,
-                "store_scales": store_scales}
+        emit = {"load": load, "constant": constant, "warm_up": warm_up, "sort": sort, "turn": turn, "copy_out": copy_out,
+                "quantise": quantise, "product": product, "exp": exp, "ln": ln, "store_y": store_y, "cast": cast,
+                "quantise_y": quantise_y, "store_words": store_words, "store_scales": store_scales}
         for step in schedule():
             emit[step[0]](*step[1:])

from contextlib import ExitStack

import concourse.mybir as mybir
from concourse.masks import make_identity

T, D, E = 1536, 1024, 2048
FLOPS = 2 * T * D * E

F32 = mybir.dt.float32
BF16 = mybir.dt.bfloat16
I32 = mybir.dt.int32
U32 = mybir.dt.uint32
U8 = mybir.dt.uint8
FP8X4 = mybir.dt.float8_e4m3fn_x4
ACT = mybir.ActivationFunctionType

P = 128
PACK = 4
PASSES = D // (P * PACK)
CHUNK = 512
HALF = CHUNK // 2
GROUP = P * PACK
GROUPS = E // GROUP
LAST = GROUPS - 1
BANKS = 8
QUADRANT = 32
SCALE_ROWS = 4

SORTED_BUFS = 6
TURNED_BUFS = 4
Y_BF_BUFS = 3
WARM_UP = 16

ORDER = "hhwwhhwwhh" + "hhwwhhhh" + "w" * 10
BLOCKS = [(kind, ORDER[:n].count(kind)) for n, kind in enumerate(ORDER)]
SINGLE_LOADS = 4
COPIER = "V" + "A" * 8 + "V" * 19
EARLY = 768

Y_CUTS = [[0, EARLY, T], [0, T], [0, T], [0, CHUNK, 2 * CHUNK, T]]
Y_REUSE = {(LAST, 0): (0, 0), (LAST, CHUNK): (0, EARLY)}

LETTER = {"turn": "t", "product": "m", "warm_up": "w", "copy_out": "e", "exp": "x", "ln": "l", "constant": "k",
          "sort": "s", "quantise": "q", "cast": "c", "quantise_y": "y", "load": "L", "store_y": "Y",
          "store_words": "W", "store_scales": "S"}
QUEUES = {
    "sync": "L" * 16 + "YYYYW" + "YYYY" + "YYYYW" + "YYYYWW" + "YYYY" + "YYW" + "YYWWS",
    "tensor": "wttttttmttttmmmmmmmmm" + "t" * 8 + "m" * 8 + "tttt" + "m" * 15 + "tt" + "m" * 9 + "tttt" + "m" * 12,
    "scalar": "eeeeexeeexxxxxxxxx|llll|" + "x" * 32 + "|" + "l" * 12 + "|" + "x" * 12 + "|" + "l" * 8,
    "vector": "ksssesqqssqqssssqqqeqqq" + "sssssseeesqqseeeqqessessqqqqsseeeeqqcqqeqceyqy" + "sssseeqeqeqq"
    + "ccyy" + "ccycyy" * 2 + "cy" * 2 + "ccyy",
}


def chunks(weights):
    return [(w, a, a + CHUNK) for w in weights for a in range(0, T, CHUNK)]


def ln_rows(g, a, b):
    return [("ln", g, t, t + 1, a, b) for t in range(PACK)]


def planes(g, cuts):
    return [("cast", g, a, b) for a, b in zip(cuts, cuts[1:])] + [("store_words", g, cuts[0], cuts[-1])]


def phases():
    first = range(PACK)
    thirds = [0, CHUNK, 2 * CHUNK, T]
    products_1 = [(w, a, a + HALF) for a in (0, HALF) for w in (0, 1)] + [(w, 0, CHUNK) for w in (2, 3)]
    products_1 += [(w, CHUNK, EARLY) for w in first]
    after_1 = ln_rows(0, 0, EARLY) + planes(0, [0, CHUNK, EARLY])
    products_2 = [(w, EARLY, 2 * CHUNK) for w in first] + [(w, a, a + CHUNK) for w in (4, 5) for a in (0, CHUNK)]
    products_2 += [(w, 2 * CHUNK, T) for w in range(6)] + chunks(range(6, PACK * LAST))
    after_2 = ln_rows(0, EARLY, T) + planes(0, [EARLY, 2 * CHUNK, T])
    for g in range(1, LAST):
        after_2 += ln_rows(g, 0, T) + planes(g, thirds)
    after_3 = ln_rows(LAST, 0, CHUNK) + planes(LAST, thirds[:2])
    for cuts in (thirds[1:3], [2 * CHUNK, T - HALF, T]):
        after_3 += [("ln", LAST, t, t + 2, cuts[0], cuts[-1]) for t in (0, 2)] + planes(LAST, cuts)
    after_3 += [("store_scales",)]
    return [(products_1, after_1), (products_2, after_2), (chunks(range(PACK * LAST, PACK * GROUPS)), after_3)]


def y_piece(g, a):
    n = max(j for j, cut in enumerate(Y_CUTS[g]) if cut <= a)
    return Y_CUTS[g][n], Y_CUTS[g][n + 1]


def steps_and_needs():
    steps, needs = [], {}

    def add(step, before):
        steps.append(step)
        needs[step] = before

    def meeting(kind, g, a, b):
        return [s for s in steps if s[0] == kind and s[1] == g and s[-2] < b and s[-1] > a]

    for n in list(range(SINGLE_LOADS)) + list(range(SINGLE_LOADS, len(BLOCKS), 2)):
        add(("load", n), [])
    add(("constant",), [])
    add(("warm_up",), [("constant",)])
    for n in range(len(BLOCKS)):
        load = ("load", n if n < SINGLE_LOADS else n - n % 2)
        add(("sort", n), [load] + [("turn", j) for j in range(n - SORTED_BUFS + 1)])
        add(("turn", n), [("sort", n)])
        add(("copy_out", n), [("turn", n)] + [("quantise", j) for j in range(n - TURNED_BUFS + 1)])
        add(("quantise", n), [("copy_out", n)])
    for products, after in phases():
        for w, a, b in products:
            operands = [("w", w)] + [("h", j) for j in range(a // P, b // P)]
            add(("product", w, a, b), [("quantise", BLOCKS.index(x)) for x in operands])
            readers = []
            if (w // PACK, a) in Y_REUSE:
                g, start = Y_REUSE[(w // PACK, a)]
                readers = meeting("store_y", g, *y_piece(g, start)) + meeting("cast", g, *y_piece(g, start))
            add(("exp", w, a, b), [("product", w, a, b)] + readers)
        for step in after:
            kind = step[0]
            if kind == "ln":
                g, t0, t1, a, b = step[1:]
                add(step, [s for t in range(t0, t1) for s in meeting("exp", PACK * g + t, a, b)])
                add(("store_y",) + step[1:], [step])
            elif kind == "cast":
                earlier = [s for s in steps if s[0] == "quantise_y"]
                add(step, meeting("ln", *step[1:]) + earlier[: max(0, len(earlier) - Y_BF_BUFS + 1)])
                add(("quantise_y",) + step[1:], [step])
            elif kind == "store_words":
                add(step, meeting("quantise_y", *step[1:]))
            else:
                add(step, [s for s in steps if s[0] == "quantise_y"])
    return steps, needs


def engine_of(step):
    if step[0] == "copy_out":
        return "scalar" if COPIER[step[1]] == "A" else "vector"
    return [engine for engine, letters in QUEUES.items() if LETTER[step[0]] in letters][0]


def schedule():
    steps, needs = steps_and_needs()
    queues = {}
    for engine, letters in QUEUES.items():
        left = [s for s in steps if engine_of(s) == engine]
        queues[engine] = []
        for letter in letters.replace("|", ""):
            step = [s for s in left if LETTER[s[0]] == letter][0]
            left.remove(step)
            queues[engine].append(step)
        assert not left
    fills = queues["tensor"]
    for old, step in zip(fills, fills[BANKS:]):
        if old[0] != "warm_up":
            needs[step].append(("copy_out" if old[0] == "turn" else "exp",) + old[1:])
    order = []
    while len(order) < len(steps):
        before = len(order)
        for queue in queues.values():
            while queue and all(s in order for s in needs[queue[0]]):
                order.append(queue[0])
                queue.remove(queue[0])
        assert len(order) > before
    return order


def tile_ssm_channel_softplus_g2_kernel(tc, h, w_in, b_in, out_0, out_1, out_2):
    nc = tc.nc
    with ExitStack() as ctx:
        sb = ctx.enter_context(tc.tile_pool(name="sb", bufs=1))
        ps = ctx.enter_context(tc.psum_pool(name="ps", bufs=1))
        ctx.enter_context(tc.manual_schedule())

        bias_bf = sb.tile([P, GROUPS, PACK], BF16, name="bias_bf")
        bias = sb.tile([P, GROUPS, PACK], F32, name="bias")
        nc.scalar.dma_start(out=bias_bf[:], in_=b_in.rearrange("(g p t) -> p g t", p=P, t=PACK))

        ident = sb.tile([P, P], F32, name="ident")
        make_identity(nc, ident[:])
        nc.gpsimd.tensor_copy(out=bias[:], in_=bias_bf[:])

        const = sb.tile([P, P * PACK], BF16, name="const", align_bytes=64)
        const_codes = sb.tile([P, P], U32, name="const_codes", align_bytes=64)
        const_scales = sb.tile([P, P], U8, name="const_scales", align_bytes=64)
        const_exp = sb.tile([P, 1], F32, name="const_exp")

        h_codes = sb.tile([P, PASSES, T], U32, name="h_codes", align_bytes=64)
        h_scales = sb.tile([P, PASSES, T], U8, name="h_scales", align_bytes=64)
        w_codes = sb.tile([P, GROUPS * PACK, PASSES, P], U32, name="w_codes", align_bytes=64)
        w_scales = sb.tile([P, GROUPS * PACK, PASSES, P], U8, name="w_scales", align_bytes=64)
        y_words = [sb.tile([P, T], U32, name="y_words%d" % g, align_bytes=64) for g in range(GROUPS)]
        y_scales = sb.tile([P, T], U8, name="y_scales", align_bytes=64)

        raw, ordered, turned, filled, y, y_bf = {}, {}, {}, {}, {}, {}

        def next_bank(user):
            filled[user] = ps.tile([P, CHUNK], F32, name="bank%d" % (len(filled) % BANKS))
            return filled[user]

        def y_part(g, t0, t1, a, b):
            start, end = y_piece(g, a)
            if (g, start) not in y:
                y[(g, start)] = sb.tile([P, PACK, end - start], F32, name="y%d_%d" % Y_REUSE.get((g, start), (g, start)))
            return y[(g, start)][:, t0:t1, a - start : b - start]

        def load(n):
            kind, j = BLOCKS[n]
            count = 1 if n < SINGLE_LOADS else 2
            if n % 2 == 0:
                raw[n // 2] = sb.tile([P, 2, D], BF16, name="raw%d" % n)
            if kind == "h":
                rows = h[P * j : P * (j + count), :].rearrange("(s m) k -> m s k", s=count)
            else:
                g, t = j // PACK, j % PACK
                rows = w_in[GROUP * g : GROUP * (g + 1), :].rearrange("(m t) k -> m t k", t=PACK)[:, t : t + count, :]
            nc.sync.dma_start(out=raw[n // 2][:, n % 2 : n % 2 + count, :], in_=rows)

        def constant():
            nc.vector.memset(const[:].bitcast(F32), 1.0)
            nc.scalar.activation(out=const_exp[:], in_=const[:].bitcast(F32)[:, 0:1], func=ACT.Exp)
            nc.vector.quantize_mx(out=const_codes[:].bitcast(FP8X4), scales=const_scales[:], in_=const[:])

        def warm_up():
            bank = next_bank("warm_up")
            for repeat in range(WARM_UP):
                nc.tensor.matmul_mx(
                    out=bank[:, 0:P],
                    lhsT=const_codes[:].bitcast(FP8X4),
                    lhsT_scale=const_scales[:],
                    rhs=const_codes[:].bitcast(FP8X4),
                    rhs_scale=const_scales[:],
                    start=True,
                    stop=True,
                )

        def sort(n):
            ordered[n] = sb.tile([P, 2, D // 32, 16], BF16, name="ordered%d" % (n % SORTED_BUFS))
            rows = raw[n // 2][:, n % 2, :]
            nc.vector.tensor_copy(out=ordered[n][:], in_=rows.rearrange("p (j u r) -> p u j r", u=2, r=16))

        def turn(n):
            words = ordered[n][:].rearrange("p u j r -> p (u j r)").bitcast(F32)
            bank = next_bank(n)
            for quarter in range(2 * PASSES):
                cols = slice(P * quarter, P * (quarter + 1))
                nc.tensor.transpose(bank[:, cols], words[:, cols], ident[:])

        def copy_out(n):
            turned[n] = sb.tile([P, PASSES, P * PACK], BF16, name="turned%d" % (n % TURNED_BUFS), align_bytes=64)
            src = filled[n][:].rearrange("p (u c m) -> p c m u", u=2, m=P)
            dst = turned[n][:].bitcast(F32).rearrange("p c (m u) -> p c m u", u=2)
            if COPIER[n] == "A":
                nc.scalar.copy(out=dst, in_=src)
            else:
                nc.vector.tensor_copy(out=dst, in_=src)

        def quantise(n):
            kind, j = BLOCKS[n]
            if kind == "h":
                cols = slice(P * j, P * (j + 1))
                for c in range(PASSES):
                    nc.vector.quantize_mx(
                        out=h_codes[:, c, cols].bitcast(FP8X4), scales=h_scales[:, c, cols], in_=turned[n][:, c, :]
                    )
            else:
                nc.vector.quantize_mx(
                    out=w_codes[:, j, :, :].rearrange("p c m -> p (c m)").bitcast(FP8X4),
                    scales=w_scales[:, j, :, :].rearrange("p c m -> p (c m)"),
                    in_=turned[n][:].rearrange("p c x -> p (c x)"),
                )

        def product(w, a, b):
            bank = next_bank((w, a))
            for c in range(PASSES):
                nc.tensor.matmul_mx(
                    out=bank[:, 0 : b - a],
                    lhsT=w_codes[:, w, c, :].bitcast(FP8X4),
                    lhsT_scale=w_scales[:, w, c, :],
                    rhs=h_codes[:, c, a:b].bitcast(FP8X4),
                    rhs_scale=h_scales[:, c, a:b],
                    start=(c == 0),
                    stop=(c == PASSES - 1),
                )

        def exp(w, a, b):
            g, t = w // PACK, w % PACK
            nc.scalar.activation(
                out=y_part(g, t, t + 1, a, b).rearrange("p t m -> p (t m)"),
                in_=filled[(w, a)][:, 0 : b - a],
                func=ACT.Exp,
                bias=bias[:, g, t : t + 1],
            )

        def ln(g, t0, t1, a, b):
            part = y_part(g, t0, t1, a, b)
            nc.scalar.activation(out=part, in_=part, func=ACT.Ln, bias=1.0)

        def store_y(g, t0, t1, a, b):
            rows = out_0[GROUP * g : GROUP * (g + 1), :].rearrange("(p t) m -> p t m", t=PACK)
            nc.sync.dma_start(out=rows[:, t0:t1, a:b], in_=y_part(g, t0, t1, a, b))

        def cast(g, a, b):
            tile = sb.tile([P, CHUNK * PACK], BF16, name="y_bf%d" % (len(y_bf) % Y_BF_BUFS), align_bytes=64)
            y_bf[(g, a)] = tile[:, 0 : (b - a) * PACK]
            nc.vector.tensor_copy(
                out=y_bf[(g, a)].rearrange("p (m r t) -> p m t r", r=4, t=PACK),
                in_=y_part(g, 0, PACK, a, b).rearrange("p t (m r) -> p m t r", r=4),
            )

        def quantise_y(g, a, b):
            nc.vector.quantize_mx(
                out=y_words[g][:, a:b].bitcast(FP8X4), scales=y_scales[SCALE_ROWS * g :, a:b], in_=y_bf[(g, a)]
            )

        def store_words(g, a, b):
            words = out_1.rearrange("g p m t -> g p (m t)").bitcast(I32)
            nc.sync.dma_start(out=words[g, :, a:b], in_=y_words[g][:, a:b].bitcast(I32))

        def store_scales():
            for q in range(P // QUADRANT):
                nc.sync.dma_start(
                    out=out_2[:, SCALE_ROWS * q : SCALE_ROWS * (q + 1), :].bitcast(I32),
                    in_=y_scales[QUADRANT * q : QUADRANT * q + SCALE_ROWS * GROUPS, :].bitcast(I32),
                )

        emit = {"load": load, "constant": constant, "warm_up": warm_up, "sort": sort, "turn": turn, "copy_out": copy_out,
                "quantise": quantise, "product": product, "exp": exp, "ln": ln, "store_y": store_y, "cast": cast,
                "quantise_y": quantise_y, "store_words": store_words, "store_scales": store_scales}
        for step in schedule():
            emit[step[0]](*step[1:])
